import numpy as np, ml_dtypes
CORES = [36,164,52,180,100,228,116,244]
N = 8
BF = ml_dtypes.bfloat16
def gentries(a):
    return np.ascontiguousarray(a.reshape(8, 16, -1).transpose(0, 2, 1)).reshape(8, -1)
def gtable(e):
    e = np.asarray(e); return np.ascontiguousarray(e.reshape(8, -1, 16).transpose(0, 2, 1)).reshape(128, -1).astype(np.int32)
T, C, RO = 1024, 96, 2
M = 3 * T
S = (N - 1) * C
def glue(rng, w, free, slots):
    o = rng.permutation(free); n = len(slots); w[o[:n]] = M + slots; p = o[n:]
    if len(p) % 2:
        w[p[-1]] = p[-1]; p = p[:-1]
    w[p[0::2]] = p[1::2]; w[p[1::2]] = p[0::2]
def sends(w):
    at = np.zeros(S, np.int64); b = np.nonzero(w >= M)[0]; at[w[b] - M] = b
    return np.concatenate([at[(N - d - 1) * C:(N - d) * C] for d in range(1, N)])
def parts(rng):
    w = np.zeros((N, 8, M), np.int64); s = np.zeros((N, 8, S), np.int64)
    for q in range(N):
        for g in range(8):
            glue(rng, w[q, g], np.arange(M), rng.permutation(S)); s[q, g] = sends(w[q, g])
    amp = rng.choice(np.array([60.0, 150.0, 255.0]), (N, 8, 16, 1))
    X = np.rint(amp * (2 * rng.random((N, 8, 16, M)) - 1)).astype(np.int64)
    return X, w, s
def plant(rng, X, h, g):
    z = rng.integers(40, 251, (16, len(h))) * rng.choice(np.array([-1, 1]), (16, len(h)))
    for e, v in ((h, z), (g, -z)):
        X[:, e] = v; X[:, (e + T) % M] = -v; X[:, (e + 2 * T) % M] = rng.integers(-3, 4, z.shape)
def twice(rng, X, h, g):
    z = rng.choice(np.array([-1, 1]), (16, len(h))); v = rng.integers(50, 61, z.shape)
    for e, y in ((h, z), (g, -z)):
        X[:, e] = y * rng.integers(230, 251, z.shape); X[:, (e + T) % M] = rng.integers(-3, 4, z.shape); X[:, (e + 2 * T) % M] = y * v
def rivals(rng, X, w):
    n = T // 8; k = np.arange(n); o = rng.permutation(T)[:3 * n].reshape(3, n); m = k % 3; i = np.arange(16)[:, None]
    z = rng.choice(np.array([-1, 1]), (16, n)); p = rng.integers(200, 251, (16, n)); u = rng.integers(0, 101, (16, n)); used = []
    X[:, m * T + o[0]] = -z * p; X[:, ((m + 1) % 3) * T + o[0]] = -z * p; X[:, ((m + 2) % 3) * T + o[0]] = z * rng.integers(200, 256, (16, n))
    for j, few, v in ((1, (k // 3) % 5, u), (2, (k // 15) % 5, np.concatenate([u[:4], u[:3:-1]]))):
        h = ((m + j) % 3) * T + o[0]; e = rng.integers(0, 3, n) * T + o[j]; w[h] = e; w[e] = h; used += [h, e]
        y = z * (1 - 2 * (i % 2)) * rng.integers(240, 256, (16, n))
        X[:, e] = y; X[:, (e + T) % M] = -y; X[:, (e + 2 * T) % M] = z * (np.where(i < 4, (i < few).astype(np.int64), v) - p)
    glue(rng, w, np.setdiff1d(np.arange(M), np.concatenate(used)), rng.permutation(S))
def pack(X, w, s):
    return {"x": np.ascontiguousarray(X.reshape(N, 128, M)).astype(np.float32).astype(BF), "twn": w.astype(np.int32), "snd": np.stack([gtable(a) for a in s])}
def setup_inputs(rng):
    return pack(*parts(rng))
def setup_inputs_ties(rng):
    X, w, s = parts(rng)
    for g in range(8):
        if g % 4 == 0:
            X[:, g] = rng.integers(-255, 256, (1, 16, 1)); live = rng.permutation(16)[:3]
            X[:, g, live] = rng.integers(0, 2, (N, 3, M))
        elif g % 4 == 1: X[:, g] = 255 * (2 * rng.integers(0, 2, (N, 16, M)) - 1)
        elif g % 4 == 2: X[:, g] = rng.integers(-1, 2, (N, 16, M))
        else: X[:, g] = rng.integers(-255, 256, (N, 16, 1))
    for q in range(N):
        for g in (5, 6):
            rivals(rng, X[q, g], w[q, g]); s[q, g] = sends(w[q, g])
    return pack(X, w, s)
def setup_inputs_ends(rng):
    X, w, s = parts(rng)
    for q in range(N):
        glue(rng, w[q, 0], np.arange(M), np.zeros(0, np.int64))
        w[q, 1] = M + rng.integers(0, S, M)
        o = rng.permutation(M); w[q, 2, o[:T]] = o[:T]; glue(rng, w[q, 2], o[T:], rng.permutation(S))
        t = rng.permutation(T)[:T // 4]; w[q, 3, t] = T + t; w[q, 3, T + t] = t
        glue(rng, w[q, 3], np.setdiff1d(np.arange(M), np.concatenate([t, T + t])), rng.permutation(S))
        o = rng.permutation(T).reshape(2, -1)
        for i in range(3):
            a = i * T + o[0]; b = ((3 - i) % 3) * T + o[1]; w[q, 4, a] = b; w[q, 4, b] = a
        glue(rng, w[q, 5], np.arange(M), rng.choice(np.array([0, C - 1, S - 1]), T))
        w[q, 6, 0] = M - 1; w[q, 6, M - 1] = 0; glue(rng, w[q, 6], np.arange(1, M - 1), rng.permutation(S)); plant(rng, X[q, 6], np.array([0]), np.array([M - 1]))
    s[:, 0::2] = rng.choice(np.array([0, T - 1, T, 2 * T - 1, 2 * T, M - 1]), (N, 4, S)); s[:, 1::2] = rng.integers(0, M, (N, 4, S))
    return pack(X, w, s)
def setup_inputs_whirl(rng):
    X, w, s = parts(rng)
    for q in range(N):
        for g in range(8):
            o = rng.permutation(T).reshape(2, -1); p = rng.integers(0, 3, o.shape) * T + o; h, e = p[0], p[1]
            w[q, g, h] = e; w[q, g, e] = h; rest = np.setdiff1d(np.arange(M), p.reshape(-1))
            if g in (2, 6):
                b = rng.permutation((p.reshape(-1) + T) % M)[:S]
                glue(rng, w[q, g], b, rng.permutation(S)); glue(rng, w[q, g], np.setdiff1d(rest, b), np.zeros(0, np.int64))
                twice(rng, X[q, g], h, e)
            else:
                glue(rng, w[q, g], rest, rng.permutation(S))
                n = T // 2 if g % 2 == 0 else T // 4
                plant(rng, X[q, g], h[:n], e[:n])
            s[q, g] = sends(w[q, g])
        X[q, 7] = rng.integers(-255, 256, (16, 1))
    return pack(X, w, s)
def setup_inputs_mesh(rng):
    X, w, s = parts(rng); K = T // 32; cell = np.arange(16 * K).reshape(16, K)
    left = np.roll(cell, 1, axis=1).ravel(); down = np.roll(cell, -1, axis=0); right = np.roll(cell, -1, axis=1).ravel(); far = np.roll(down, -1, axis=1).ravel()
    down = down.ravel(); row = np.repeat(np.arange(16), K); col = np.tile(np.arange(K), 16); cell = cell.ravel()
    a = 2 * cell; b = a + 1; w0 = np.zeros(M, np.int64); org = np.zeros(M, np.int64)
    w0[2 * T + a] = b; w0[b] = 2 * T + a
    bl = 2 * left + 1; w0[a] = T + bl; w0[T + bl] = a
    bd = 2 * down + 1; w0[T + a] = 2 * T + bd; w0[2 * T + bd] = T + a
    org[a] = cell; org[T + a] = down; org[2 * T + a] = far; org[b] = cell; org[T + b] = far; org[2 * T + b] = right
    low = np.nonzero(w0 > np.arange(M))[0]; tri = np.arange(M) % T; side = np.arange(M) // T
    for q in range(N):
        for g in range(8):
            place = rng.permutation(T); turn = rng.integers(0, 3, T); ren = ((side + turn[tri]) % 3) * T + place[tri]
            w[q, g, ren] = ren[w0]; c = rng.permutation(low)[:S // 2]; c = np.concatenate([c, w0[c]]); w[q, g, ren[c]] = M + rng.permutation(S)
            v = 120 * np.sin(rng.random((16, 1)) * row + rng.random((16, 1)) * col + 6 * rng.random((16, 1))) + 40 * rng.standard_normal((16, 16 * K))
            X[q, g][:, ren] = np.clip(np.rint(v), -255, 255).astype(np.int64)[:, org]; s[q, g] = sends(w[q, g])
    return pack(X, w, s)
def setup_inputs_spread(rng):
    X, w, s = parts(rng)
    X = np.exp2(8 * rng.random((N, 8, 1, M))) * (rng.random((N, 8, 1, M)) > 0.0625) * (2 * rng.random((N, 8, 16, M)) - 1)
    X = np.clip(np.rint(X), -255, 255).astype(np.int64)
    for q in range(N):
        for g in range(8):
            glue(rng, w[q, g], np.arange(M), (S * rng.random(int(rng.integers(0, T))) ** 2).astype(np.int64))
    return pack(X, w, (M * rng.random((N, 8, S)) ** 3).astype(np.int64))
def check_inputs(d):
    bad = []; v = np.asarray(d["x"]).astype(np.float32); w = np.asarray(d["twn"]).astype(np.int64)
    if not (np.all(v == np.rint(v)) and np.all(np.abs(v) <= 255)): bad.append("whole numbers of x")
    for k, hi in (("twn", M + S - 1), ("snd", M - 1)):
        if np.min(d[k]) < 0 or np.max(d[k]) > hi: bad.append("range of " + k)
    back = np.take_along_axis(w, np.clip(w, 0, M - 1), 2)
    if np.any((w < M) & (back != np.arange(M))): bad.append("twins of twins in twn")
    return bad
def reference(x, twn, snd):
    X = x.astype(np.float32).astype(np.int32).reshape(N, 8, 16, M); tw = twn.astype(np.int64)
    sl = np.stack([gentries(a) for a in snd]).astype(np.int64)
    h = np.arange(M); nx = (h + T) % M; pv = (h + 2 * T) % M
    for rnd in range(RO):
        give = np.take_along_axis(X, pv[sl][:, :, None, :], 3)
        come = np.stack([np.concatenate([give[(a - d) % N][..., (d - 1) * C:d * C] for d in range(1, N)], axis=2) for a in range(N)])
        own = tw < M; t = np.minimum(tw, M - 1)
        D = np.take_along_axis(np.concatenate([X, come], axis=3), np.where(own, pv[t], tw)[:, :, None, :], 3)
        far = X[..., pv]
        gain = np.sum((X - X[..., nx]) ** 2 - (far - D) ** 2, axis=2)
        gain = np.where(own & (t % T != h % T), gain, 0).reshape(N, 8, 3, T)
        best = np.argmax(gain, axis=2)
        took = ((np.arange(3)[:, None] == best[:, :, None, :]) & (gain > 0)).reshape(N, 8, M)
        flip = took & own & np.take_along_axis(took, t, 2)
        Y = np.where(own[:, :, None, :], far, np.maximum(far, D))[..., nx]
        fn = flip[..., pv]; fp = flip[..., nx]
        loc = np.where(fn, pv[t][..., pv], np.where(fp, pv, h)); src = np.where(fn, nx, np.where(fp, nx[t][..., nx], h))
        X = np.take_along_axis(Y, np.where(flip, pv[t], src)[:, :, None, :], 3)
        e = np.take_along_axis(tw, src, 2)
        tw = np.where(e < M, np.take_along_axis(loc, np.minimum(e, M - 1), 2), e)
        sl = np.take_along_axis(loc, sl, 2)
    return {"yx": X.reshape(N, 128, M).astype(np.float32).astype(BF), "yt": tw.astype(np.float32)}

@@ -1,0 +1,431 @@
+from concourse.bass import DstId, RemoteDMATransfer
+from concourse.mybir import AluOpType as A, ActivationFunctionType as F
+
+TR, M, S, C, N = 1024, 3072, 672, 96, 8
+W = M + S
+WC = W // 16
+BIG = float(2 ** 25)
+R16, R1K = 1.5 * 2 ** 27, 1.5 * 2 ** 33
+SCALES = [1.0, -1.0, -BIG, 1536.0, 1024.0, -1024.0, 219.0, float(WC), 1.0 / 16]
+
+
+def _sb(dt, **k):
+    return {n: ("sbuf", [128] + (v if isinstance(v, list) else [v]), dt) for n, v in k.items()}
+
+
+SCRATCH = {}
+SCRATCH.update(_sb("bfloat16", O=W, O2=M, YO=M, DM=M, come0=16 + S, come1=16 + S, give0=S, give1=S, WB=W, U=W,
+                   same=192, bord=192, sgn=192, b16=304, low=304, ci=64, c16=256, cl=192, ones=192, sel=WC, hi=WC, lo=WC, hi2=WC, lo2=WC,
+                   Ib=128 * (len(SCALES) + 1), Bs=144, Bh=144, Bl=144, dh=192, dw=192))
+SCRATCH.update(_sb("float32", SD=M, SL=W, TF=[6, 2, 16], TW=192, f1=192, f2=192, MA=192, MB=192, N1=192, N2=192, PG=192,
+                   XL=192, EL=192, TS=192, LOC=WC, sm=192, phi=64, Z=[3, 8, 2, 8], col=12, RD=256, RC=8, base=256,
+                   If=256, EE=64, GI=16))
+SCRATCH.update(_sb("int32", TB=[2, 6, 16], SN=42, i1=42, i2=42, P=8))
+SCRATCH.update(_sb("uint16", dl=192, yl=192, xl=192, el=WC, sl=42, pl=64))
+PSUM = ("A0", "A1", "G0", "G1", "G2", "KK", "AB", "PT")
+for _n in PSUM:
+    SCRATCH[_n] = ("psum", [128, 512], "float32")
+NDMA = 40
+SEMAPHORES = ["cv", "ca", "cp", "cg", "arr0", "arr1", "snt0", "snt1"] + ["d%d" % _k for _k in range(NDMA)]
+PLAN = {"yact": ((2, 3, 4, 5), (3, 4, 5)), "dact": ((), (5,)), "dchunk": 512, "xchunk": 512, "ychunk": 512, "tchunk": 512, "wchunk": 512,
+        "load": 1024, "ochunk": (1024, 512), "rem": (9.0, 7.5), "f": 1.0, "gat": 1.56, "row": 0.035, "dma": 1.7}
+ORDER = ("0M4G1n1s1x4L1i1H0R4w1M2Q393e1C2B2r2w2V2G2c112Z3o3y3S553j3D3X1d423I3t512h0j0o868a8g8k0e5Y0t8v6y684B344Q6i8F8J0W1W3N8q8z2m2L94988U8Y094c5p47045k5E5J5z5T5O5u8P9e21634h0y9r9x9h9nah6H0D0I9L9R165j5e9B9H279Va1a5ab6M7U837g4m1R6d7K7TalapaBaFaJ6T777c7lb06Xawb4b96n4raVbkaObdbnbsbxbC6s724W7Hc6c17s7x7CbMbT6FdXe8cseeenetbWcKcFbLcVcQehe2ewcdcicxcCdaded1djdtdodCdIdDdNf5d6fpeCeIffeLcnfaeReXf0fGfJgNg5fkfugHfQfVfYfzhbh1gagfgigsgndWhrhxhAgxgCgXkrhahhhpkBiSj0kvkQithKi9kFkLl0kUiziFiIhGhRhUl4lpmggVlClfi5igijlMlaltljlzi0iOipj2jBj7jejNmrmxlSmmlImHk6kekgkom6mclWm2n1mBnqmL1bpEpzjsjxjGpJjijnmQmWnen5nanlnunznKnDnNnXo2nSobjSjXock2oworp5ojomq4qaqdpPpVpYoDoSoXoIoNpfqjpaqpqsplprqyqCp2qWrbqHrnrqqRrKrTr6pwqMr1sJsRszsHrxrCrFt3rgtmtvtbtdtlrWs1s6sjs9sesostuluaujuttwtFtHtPu0u9tRtZsSt1")
+
+
+def meet(x, y):
+    return x[0] == y[0] and x[1] < y[2] and y[1] < x[2] and (x[3] is None or y[3] is None or x[3] == y[3])
+
+
+def link(ops):
+    touch = {}
+    for n, o in enumerate(ops):
+        o["id"] = n
+        o["banks"] = set(r[0] for r in o["r"] + o["w"] if r[0] in PSUM)
+        near = set()
+        for r in o["r"] + o["w"]:
+            near.update(touch.get(r[0], ()))
+        o["pre"] = []
+        for m in sorted(near):
+            d = ops[m]
+            raw = any(meet(x, y) for x in o["r"] for y in d["w"])
+            war = any(meet(x, y) for x in o["w"] for y in d["w"] + d["r"])
+            bank = bool(o["banks"] & d["banks"]) and not (o["alt"] == d["alt"] and o["alt"] in "va")
+            if raw or war or bank:
+                o["pre"].append((m, raw or war))
+        for r in o["r"] + o["w"]:
+            touch.setdefault(r[0], set()).add(n)
+
+
+def emit(g, T, ops, order):
+    q = {"v": g.vector, "a": g.scalar, "p": g.tensor, "g": g, "s": g.sync}
+    know = {e: ({}, set()) for e in q}
+    assert sorted(m for m, _ in order) == list(range(len(ops)))
+    for n, (m, e) in enumerate(order):
+        o = ops[m]; o["e"] = e; o["n"] = n; deps = []
+        assert e in o["alt"] and all("n" in ops[x] for x, _ in o["pre"])
+        for x, raw in o["pre"]:
+            d = ops[x]
+            if d["kind"] == "rem" or (d["kind"] == "c" and o["kind"] == "c" and d["e"] == e and (e == "p" or not raw)):
+                continue
+            deps.append(d)
+        clk, dm = know[e]; o["waits"] = []
+        for d in sorted(deps, key=lambda d: -d["n"]):
+            if (d["n"] in dm) if d["kind"] == "dma" else (clk.get(d["e"], -1) >= d["n"]):
+                continue
+            o["waits"].append(d); d["sig"] = True
+            for k, v in d["clk"].items():
+                clk[k] = max(clk.get(k, -1), v)
+            dm.update(d["dm"])
+        o["clk"] = dict(clk); o["dm"] = set(dm)
+        if o["kind"] == "dma":
+            o["dm"].add(n)
+        else:
+            o["clk"][e] = n
+    count = {e: 0 for e in q}; nd = 0; seen = set()
+    for m, e in order:
+        o = ops[m]; best = {}
+        for d in o["waits"]:
+            best[d["at"][0]] = max(best.get(d["at"][0], 0), d["at"][1])
+        for s, v in o["ext"]:
+            if (e, s) not in seen:
+                seen.add((e, s)); best[s] = v
+        for s, v in best.items():
+            q[e].wait_ge(T.sem[s], v)
+        ins = o["fn"](q[e], e)
+        if o["kind"] == "dma":
+            o["at"] = ("d%d" % nd, 16); nd += 1
+            ins.then_inc(T.sem[o["at"][0]], 16)
+        elif o.get("sig"):
+            count[e] += 1; o["at"] = ("c" + e, count[e])
+            ins.then_inc(T.sem["c" + e], 1)
+    for m, e in order:
+        if ops[m]["kind"] == "dma" and not ops[m].get("sig"):
+            g.sync.wait_ge(T.sem[ops[m]["at"][0]], 16)
+
+
+def calls(core, rank, T, topo, plan):
+    ops = []
+
+    def R(name, lo, hi, step=1, row=None):
+        part = slice(0, 128) if row is None else slice(row, 128, 16)
+        ap = T[name][part, lo:hi] if step == 1 else T[name][part, lo:hi:step]
+        return (ap, [(name, lo, hi, row)], len(range(lo, hi, step)), 4 if SCRATCH[name][2].endswith("32") else 2)
+
+    def ind(win, off):
+        return (win[0].indirect(off[0]), win[1] + off[1], 16 * off[2], 0)
+
+    def add(e, kind, fn, w, r, c, lat=0.0, ext=()):
+        ops.append({"e": e[0], "alt": e, "kind": kind, "fn": fn, "w": list(w), "r": list(r), "ext": list(ext), "c": c, "lat": lat})
+
+    def cost(out, a, cycles=1.0):
+        return 0.05 + 0.83e-3 * plan["f"] * (plan["gat"] * a[2] if a[3] == 0 else max(64, out[2] * cycles))
+
+    def tt(out, a, b, op, ext=()):
+        both = a[1][0][0] not in PSUM and b[1][0][0] not in PSUM
+        add("v", "c", lambda q, e: q.tensor_tensor(out[0], a[0], b[0], op), out[1], a[1] + b[1], cost(out, a, 2 if both else 1), 0.0, ext)
+
+    def ts(out, a, s1, op0, s2=None, op1=None):
+        r = list(a[1]); v = []
+        for s in (s1, s2):
+            if isinstance(s, tuple):
+                r += s[1]; v.append(s[0])
+            else:
+                v.append(s)
+        if op1 is None:
+            add("v", "c", lambda q, e: q.tensor_scalar(out[0], a[0], v[0], None, op0), out[1], r, cost(out, a))
+        else:
+            add("v", "c", lambda q, e: q.tensor_scalar(out[0], a[0], v[0], v[1], op0, op1), out[1], r, cost(out, a))
+
+    def cp(out, a, e="v", ext=()):
+        add(e, "c", lambda q, e: q.tensor_copy(out[0], a[0]) if e == "v" else q.activation(out[0], a[0], F.Copy), out[1], a[1],
+            cost(out, a, 0.5 if e == "v" and out[3] == a[3] == 2 else 1), 0.0, ext)
+
+    def act(out, a, func, scale=1.0, bias=None):
+        if bias is None:
+            add("a", "c", lambda q, e: q.activation(out[0], a[0], func, scale=scale), out[1], a[1], cost(out, a))
+        else:
+            add("a", "c", lambda q, e: q.activation(out[0], a[0], func, bias=bias, scale=scale), out[1], a[1], cost(out, a))
+
+    def scale(out, a, c):
+        add("av", "c", lambda q, e: q.tensor_scalar(out[0], a[0], c[0], None, A.mult) if e == "v"
+            else q.activation(out[0], a[0], F.Copy, scale=c[0]), out[1], a[1] + c[1], cost(out, a))
+
+    def group(out, terms, start=True, stop=True):
+        def fn(q, e):
+            for k, t in enumerate(terms):
+                ins = q.matmul((t[2] if len(t) > 2 else out)[0], t[0][0], t[1][0], start and k == 0, stop and k == len(terms) - 1)
+            return ins
+        add("p", "c", fn, out[1], sum((t[0][1] + t[1][1] for t in terms), []),
+            sum(0.417e-3 * plan["f"] * max(64, t[1][2]) * (4 if t[0][3] == 4 else 1) for t in terms))
+
+    def ms(out, c):
+        add("v", "c", lambda q, e: q.memset(out[0], c), out[1], [], cost(out, out, out[3] / 4))
+
+    def iota(out, pat, base=0, cm=0, small=True):
+        c = 0.13 + 1.66e-3 * out[2]
+        if small:
+            add("g", "c", lambda q, e: q.iota(out[0], pat, base, cm, allow_small_or_imprecise_dtypes=True), out[1], [], c)
+        else:
+            add("g", "c", lambda q, e: q.iota(out[0], pat, base, cm), out[1], [], c)
+
+    def dma(out, a, row):
+        add("s", "dma", lambda q, e: q.dma_start(out[0], a[0]), out[1], a[1], 8 * (plan["row"] + row / 22e3), plan["dma"])
+
+    def side(name, p, n=64):
+        return R(name, p * n, (p + 1) * n)
+
+    def chunks(step, skip):
+        out = []
+        for k in range(6):
+            if k not in skip:
+                if out and out[-1][1] == 512 * k and out[-1][1] % step:
+                    out[-1][1] += 512
+                else:
+                    out.append([512 * k, 512 * k + 512])
+        return out
+
+    col = lambda k: R("col", k, k + 1)
+    Ib = lambda k: R("Ib", 128 * k, 128 * k + 128)
+    I1, IN, NB, I1536, K1, KN, I219, IW, I16, ZERO = (Ib(k) for k in range(10))
+    IF, IFN = (R("If", 128 * k, 128 * k + 128) for k in range(2))
+
+    for gl in range(2):
+        dma((T.TB[:, gl], [("TB", gl, gl + 1, None)]), (T.twn[gl:8:2, :], []), 384)
+    dma(R("SN", 0, 42), (T.snd[:, :], []), 168)
+    for lo, hi in chunks(plan["load"], ()):
+        dma(R("O", (lo + TR) % M, (lo + TR) % M + hi - lo), (T.x[:, lo:hi], []), 2 * (hi - lo))
+    for p in range(3):
+        dma(side("O2", p, TR), (T.x[:, ((p + 2) % 3) * TR:((p + 2) % 3 + 1) * TR], []), 2048)
+
+    iota(R("P", 0, 1), [[0, 1]], 0, 1, small=False)
+    iota(R("RD", 0, 256), [[1, 256]])
+    iota(R("RC", 0, 8), [[1, 8]])
+    iota(R("ones", 0, 192), [[0, 192]], 1)
+    iota(R("WB", 2048, W), [[0, W - 2048]])
+    iota(R("SL", M, W), [[0, S]])
+    ms(R("O", M, W), 0.0)
+    ts(R("P", 1, 2), R("P", 0, 1), 1, A.bitwise_and)
+    ts(R("P", 2, 3), R("P", 0, 1), 1, A.arith_shift_right)
+    ts(R("P", 3, 4), R("P", 0, 1), 4, A.arith_shift_right)
+    ts(R("P", 4, 5), R("P", 0, 1), 15, A.bitwise_and)
+    ms(ZERO, 0.0)
+    cp(R("col", 0, 5), R("P", 0, 5))
+    ts(IF, R("RD", 0, 128), col(0), A.is_equal)
+    ts(R("base", 0, 256), R("RD", 0, 256), 16.0, A.mult, col(4), A.add)
+    ts(R("GI", 0, 8), R("RC", 0, 8), col(3), A.is_equal)
+    ts(R("GI", 8, 16), R("RC", 0, 8), col(3), A.is_equal, -1.0, A.mult)
+    act(IFN, IF, F.Copy, -1.0)
+    for n, s in enumerate(SCALES):
+        act(Ib(n), IF, F.Copy, s)
+    act(R("c16", 0, 256), R("RD", 0, 256), F.Copy, 16.0)
+    ts(R("cl", 0, 192), R("ones", 0, 192), col(4), A.mult, 7.5, A.subtract)
+    ts(col(8), col(1), 0.0, A.is_equal)
+    ts(R("EE", 0, 64), R("RD", 0, 64), col(2), A.is_equal, 4.0, A.mult)
+    ts(col(5), col(3), 16.0, A.mult, 15.0, A.add)
+    ts(col(6), col(4), 0.0, A.is_equal)
+    ts(col(7), col(4), 1.0, A.is_equal, float(WC), A.mult)
+    ts(col(9), col(4), 2.0, A.is_equal, 1.0 / 16, A.mult)
+    ms(R("WB", 0, 1024), 0.0)
+    ms(R("WB", 1024, 2048), 0.0)
+    ts(R("Bs", 0, 144), R("RD", 0, 144), col(5), A.is_equal, col(6), A.mult)
+    tt(col(7), col(7), col(9), A.add)
+    ts(R("ci", 0, 64), R("ones", 0, 64), col(4), A.mult)
+    ms(R("b16", 256, 304), 0.0)
+    ms(R("low", 256, 304), 0.0)
+    ts(R("Bh", 0, 144), R("RD", 0, 144), col(5), A.is_equal, col(7), A.mult)
+    ts(col(10), col(4), 2.5, A.subtract)
+    tt(col(10), col(10), col(10), A.mult)
+    ts(col(10), col(10), 3.0, A.is_lt)
+    ts(R("Bl", 0, 144), R("RD", 0, 144), col(5), A.is_equal, col(10), A.mult)
+    for r in range(2):
+        ms(R("come%d" % r, 0, 16), -256.0)
+    for nm in ("sel", "hi", "lo"):
+        ms(R(nm, 192, WC), 0.0)
+    cp(R("LOC", 192, WC), R("base", 192, WC), "a")
+    cp(R("hi2", 0, WC), R("c16", 0, WC), "av")
+    ts(R("lo2", 0, WC), R("RD", 0, WC), 0.0, A.mult, R("cl", 0, 1), A.add)
+    dma(R("WB", 0, W, row=3), R("hi2", 0, WC), 468)
+    dma(R("WB", 0, W, row=4), R("lo2", 0, WC), 468)
+
+    for gl in range(2):
+        add("v", "c", lambda q, e, gl=gl: q.tensor_scalar(T.TF[:, :, gl, :], T.TB[:, gl], -7.5, None, A.add),
+            [("TF", 0, 2, gl)], [("TB", gl, gl + 1, None)], 0.13)
+    for b in range(6):
+        add("v", "c", lambda q, e, b=b: q.transpose(T.TW[:, b:192:6], T.TF[:, b]), [("TW", 0, 192, b)], [("TF", 0, 2, None)], 0.11)
+    cp(R("sl", 0, 42), R("SN", 0, 42))
+    ts(R("dl", 0, 192), R("TW", 0, 192), 7.5, A.add)
+    ts(R("i1", 0, 42), R("SN", 0, 42), 15, A.bitwise_and)
+    ts(R("i2", 0, 42), R("SN", 0, 42), 4, A.arith_shift_right)
+    ts(R("f2", 0, 42), R("i1", 0, 42), float(WC), A.mult)
+    tt(R("f2", 0, 42), R("f2", 0, 42), R("i2", 0, 42), A.add)
+    cp(R("el", 0, 42), R("f2", 0, 42))
+
+    TW = R("TW", 0, 192)
+    BB, AA = R("AB", 0, 192), R("AB", 192, 384)
+    k = lambda p: R(("A0", "A1", "KK")[p], 0, 64)
+    sel = lambda p: side("sel", p)
+    stage = [0]
+
+    def staging():
+        stage[0] += 1
+        return R("A%d" % (1 - stage[0] % 2), 0, 512)
+
+    def reduce(p, first):
+        nm = "SL" if first else "SD"
+        terms = [(R(nm, p * TR + j, (p + 1) * TR, 8), R("GI", 0, 8) if first else R("GI", 8, 16), R("G%d" % p, j, 64, 8)) for j in range(8)]
+        group(R("G%d" % p, 0, 64), ([(ZERO, R("ones", 0, 64))] if first else []) + terms, first, not first)
+
+    def compact(out, B, lo, hi, more=()):
+        group(out, list(more) + [(R(B, 15 - i, 143 - i), R("U", lo + i, hi, 16)) for i in range(16)])
+
+    for r in range(2):
+        come = R("come%d" % r, 0, 16 + S)
+        come = (come[0], come[1] + [("arr%d" % r, 0, 1, None)], come[2], come[3])
+        arr = [("arr%d" % r, N - 1)]
+        cp(R("give%d" % r, 0, S), ind(R("O", 0, M), R("sl", 0, 42)), "av")
+        trs = []
+        for d in range(1, N):
+            dst = T.cores[(rank + d) % N]
+            rid, pid = topo.addr(dst, core)
+            trs.append(RemoteDMATransfer(dst_ids=[DstId(rid=rid, pnc=pid)], dma_engine_mask=1 << topo.engines(core, dst)[d - 1],
+                                         remote_sem=T.sem["arr%d" % r], src=T["give%d" % r][:, (d - 1) * C:d * C],
+                                         dst=T["come%d" % r][:, 16 + (d - 1) * C:16 + d * C]))
+        add("g", "rem", lambda q, e, trs=trs, r=r: q.remote_dma_fused(trs, local_sem=T.sem["snt%d" % r]), [("arr%d" % r, 0, 1, None)],
+            [("give%d" % r, 0, S, None)], 0.3, plan["rem"][r])
+        ts(R("b16", 0, 192), TW, R16, A.add, R16, A.subtract)
+        tt(R("low", 0, 192), TW, R("b16", 0, 192), A.subtract)
+        less = [(I1, R("b16", 0, 192)), (I1, R("low", 0, 192)), (IN, R("c16", 64, 256)), (IN, R("cl", 0, 192))]
+        group(BB, less)
+        act(R("bord", 0, 192), TW, F.Relu, 1.0, 8.5 - M)
+        act(R("sgn", 0, 192), TW, F.Sign, -1.0, TR - 8.0)
+        act(R("f1", 0, 192), BB, F.Identity, 1.0, R1K)
+        act(R("f1", 0, 192), R("f1", 0, 192), F.Identity, 1.0, -R1K)
+        ts(R("yl", 0, 192), TW, 23.5 - M, A.add, 15.0, A.max)
+        tt(R("same", 0, 192), BB, R("f1", 0, 192), A.is_equal)
+        for lo, a, b in ((64, 0, 192), (0, 128, 192), (256, 0, 64)):
+            group(R("PT", lo, lo + b - a), [(IW, R("low", a, b)), (I16, R("b16", a, b)),
+                                            (I1536, R("ones", a, b)), (I219, R("ones", a, b))])
+        group(AA, less + [(I1536, R("sgn", 0, 192)), (I1536, R("ones", 0, 192))])
+        for row, nm in ((1, "low"), (2, "b16")):
+            cp(R(nm, 192, 256), R(nm, 0, 64), "av")
+            dma(R("WB", 0, W, row=row), R(nm, 64, 64 + WC), 468)
+        for p in range(3):
+            for h in range(2):
+                s = staging()
+                group(s, [(I1, side("O", 2 * ((p + 1) % 3) + h, 512)), (IN, side("O", 2 * ((p + 2) % 3) + h, 512))])
+                act(side("SL", 2 * p + h, 512), s, F.Square)
+            reduce(p, True)
+        for lo, hi in chunks(plan["dchunk"], plan["dact"][r]):
+            tt(R("SD", lo, hi), ind(R("O", 0, W), R("dl", lo // 16, hi // 16)), R("O2", lo, hi), A.subtract)
+            act(R("SD", lo, hi), R("SD", lo, hi), F.Square)
+        for n in plan["dact"][r]:
+            cp(side("DM", n, 512), ind(R("O", 0, W), side("dl", n, 32)), "a")
+            s = staging()
+            group(s, [(I1, side("DM", n, 512)), (IN, side("O", n, 512))])
+            act(side("SD", n, 512), s, F.Square)
+        for p in range(3):
+            reduce(p, False)
+            for b in range(2):
+                scale((T.Z[:, p, :, b, :], [("Z", p, p + 1, b)], 64, 4), R("G%d" % p, 0, 64), col((8, 1)[b]))
+            if p == 1:
+                ts(side("sm", 0), k(0), 3.0, A.max)
+            if p == 2:
+                tt(side("sm", 1), k(1), side("sm", 0), A.max)
+            group(k(p), [(NB, side("same", p)), (NB, side("bord", p))] + [(I1, side("ones", 0))] * (2 - p)
+                  + [((T.Z[:, p], [("Z", p, p + 1, None)], 128, 4), R("EE", 0, 64))])
+        tt(side("sm", 2), k(2), side("sm", 1), A.max)
+        for p in range(3):
+            tt(sel(p), k(p), side("sm", 2), A.is_equal)
+        dma(R("WB", 0, W, row=0), R("sel", 0, WC), 468)
+        tt(R("PG", 0, 192), R("PT", 64, 256), R("sel", 0, 192), A.mult)
+        group(R("KK", 192, 256), [(IF, side("PG", p)) for p in range(3)])
+        cp(R("pl", 0, 64), R("KK", 192, 256))
+        tt(R("MA", 0, 192), AA, R("sel", 0, 192), A.mult)
+        tt(R("MB", 0, 192), BB, R("sel", 0, 192), A.mult)
+        MA = lambda p: (IF, side("MA", p))
+        MB = lambda p: (IF, side("MB", p))
+        group(side("G0", 0), [MA(0), MB(2)] + [(I1536, sel(2))] * 2 + [(K1, sel(1))])
+        group(side("G0", 1), [MA(1), MB(0), (K1, sel(2))])
+        group(side("G0", 2), [MA(2), MB(1)] + [(KN, sel(0))] * 2)
+        group(side("G1", 0), [MA(2)] + [(K1, sel(2)), (K1, sel(1))] * 2)
+        group(side("G1", 1), [MA(0), (KN, sel(0)), (KN, sel(2))])
+        group(side("G1", 2), [MA(1), (KN, sel(1)), (KN, sel(0))])
+        tt(R("N1", 0, 192), R("PT", 0, 192), R("sel", 0, 192), A.mult)
+        tt(R("N2", 0, 192), R("PT", 128, 320), R("sel", 0, 192), A.mult)
+        for h in range(2):
+            cp(side("U", h, 512), ind(R("WB", 0, W), side("pl", h, 32)), "av")
+        compact(R("KK", 256, 320), "Bs", 0, TR)
+        compact(R("AB", 384, 448), "Bh", 0, TR, [(I1536, R("ones", 0, 64)), (I219, R("ones", 0, 64))])
+        if r == 0:
+            cp(R("dh", 0, 192), R("G1", 0, 192), "av")
+            tt(R("dw", 0, 192), R("G1", 0, 192), R("dh", 0, 192), A.subtract)
+            for nm, src, row in (("hi", "dh", 1), ("lo", "dw", 2)):
+                for q in range(3):
+                    tt(side(nm, q), R("KK", 256, 320), side(src, q), A.mult)
+                dma(R("WB", 0, W, row=row), R(nm, 0, WC), 468)
+        for lo, hi in chunks(plan["ychunk"], plan["yact"][r]):
+            tt(R("YO", lo, hi), ind(come, R("yl", lo // 16, hi // 16)), R("O", lo, hi), A.max, arr)
+        for n in plan["yact"][r]:
+            cp(side("DM", n, 512), ind(come, side("yl", n, 32)), "a", arr)
+            s = staging()
+            group(s, [(I1, side("DM", n, 512))])
+            tt(side("YO", n, 512), s, side("O", n, 512), A.max)
+        phi = R("phi", 0, 64)
+        cp(phi, R("KK", 256, 320), "av")
+        for q in range(3):
+            tt(side("XL", q), side("G0", q), phi, A.mult)
+            if r == 1:
+                tt(side("G1", q), side("G1", q), phi, A.mult)
+            tt(side("TS", q), R("AB", 384, 448), sel((q + 1) % 3), A.mult)
+        for lo, hi in ((0, 64), (64, 192)):
+            for a in range(lo, hi, 64):
+                group(R("A0", a, a + 64), [(I1, R("c16", a, a + 64)), (I1, R("ci", 0, 64)), (IF, R("XL", a, a + 64))])
+            cp(R("xl", lo, hi), R("A0", lo, hi))
+        if r == 1:
+            tt(R("LOC", 0, 192), R("G1", 0, 192), R("base", 0, 192), A.add)
+            dma(R("SL", 0, W, row=0), R("LOC", 0, WC), 936)
+        for q in range(3):
+            group(side("G2", q), [(IF, side("N1", (q + 2) % 3)), (IFN, side("N2", (q + 2) % 3)), (IFN, side("N1", (q + 1) % 3)),
+                                  (IF, side("TS", q))])
+        for q in range(3):
+            tt(side("EL", q), side("G2", q), phi, A.mult)
+        tt(R("EL", 0, 192), R("PT", 64, 256), R("EL", 0, 192), A.add)
+        cp(R("el", 42, WC), R("EL", 0, 192))
+        for lo, hi in chunks(plan["xchunk"], ()):
+            cp(R("O", lo, hi), ind(R("YO", 0, M), R("xl", lo // 16, hi // 16)), "av")
+            if hi % plan["ochunk"][r]:
+                continue
+            lo = hi - plan["ochunk"][r]
+            if r == 1:
+                at = (lo + 2 * TR) % M
+                dma((T.yx[:, at:at + hi - lo], []), R("O", lo, hi), 2 * (hi - lo))
+            else:
+                dma(R("O2", lo, hi), R("O", lo, hi), 2 * (hi - lo))
+        if r == 0:
+            cp(R("U", 0, S), ind(R("WB", 0, W), R("el", 0, 42)), "av")
+            compact(R("KK", 320, 362), "Bl", 0, S)
+            ts(R("sl", 0, 42), R("KK", 320, 362), 7.5, A.add)
+            for p, at in enumerate((R("KK", 0, 64), R("AB", 0, 64), R("PT", 320, 384))):
+                lo = S + p * TR
+                for a in range(lo, lo + TR, plan["wchunk"]):
+                    cp(R("U", a, a + plan["wchunk"]), ind(R("WB", 0, W), R("el", a // 16, (a + plan["wchunk"]) // 16)), "av")
+                compact(at, "Bl", lo, lo + TR)
+                ts(side("dl", p), at, 7.5, A.add)
+                cp(side("TW", p), at, "av")
+        else:
+            for lo, hi in chunks(plan["tchunk"], ()):
+                cp(R("SD", lo, hi), ind(R("SL", 0, W), R("el", (S + lo) // 16, (S + hi) // 16)), "av")
+                dma((T.yt[:, lo:hi], []), R("SD", lo, hi, row=0), 400)
+    link(ops)
+    return ops
+
+
+def rank_program(g, core, T, topo):
+    rank = T.rank_of(core)
+    if rank is None:
+        return
+    digits = "0123456789abcdefghijklmnopqrstuvwxyzABCDEFGHIJKLMNOPQRSTUVWXYZ"
+    code = [digits.index(ORDER[i]) * 62 + digits.index(ORDER[i + 1]) for i in range(0, len(ORDER), 2)]
+    emit(g, T, calls(core, rank, T, topo, PLAN), [(v // 5, "vapgs"[v % 5]) for v in code])
+    for r in range(2):
+        g.wait_ge(T.sem["snt%d" % r], N - 1)

@@ -4,9 +4,13 @@ from concourse.mybir import AluOpType as A, ActivationFunctionType as F
 TR, M, S, C, N = 1024, 3072, 672, 96, 8
 W = M + S
 WC = W // 16
+MID = 7.5 * WC
 BIG = float(2 ** 25)
-R16, R1K = 1.5 * 2 ** 27, 1.5 * 2 ** 33
-SCALES = [1.0, -1.0, -BIG, 1536.0, 1024.0, -1024.0, 219.0, float(WC), 1.0 / 16]
+FAR = 32768.0
+R16 = 1.5 * 2 ** 27
+SCALES = [1.0, -1.0, 0.0, float(WC), 1.0 / 16, 1024.0, -1024.0, 3072.0, -192.0]
+DUP = 2
+LISTS = ("sel", "hi", "dlo", "b16", "low")
 
 
 def _sb(dt, **k):
@@ -14,22 +18,31 @@ def _sb(dt, **k):
 
 
 SCRATCH = {}
-SCRATCH.update(_sb("bfloat16", O=W, O2=M, YO=M, DM=M, come0=16 + S, come1=16 + S, give0=S, give1=S, WB=W, U=W,
-                   same=192, bord=192, sgn=192, b16=304, low=304, ci=64, c16=256, cl=192, ones=192, sel=WC, hi=WC, lo=WC, hi2=WC, lo2=WC,
-                   Ib=128 * (len(SCALES) + 1), Bs=144, Bh=144, Bl=144, dh=192, dw=192))
-SCRATCH.update(_sb("float32", SD=M, SL=W, TF=[6, 2, 16], TW=192, f1=192, f2=192, MA=192, MB=192, N1=192, N2=192, PG=192,
-                   XL=192, EL=192, TS=192, LOC=WC, sm=192, phi=64, Z=[3, 8, 2, 8], col=12, RD=256, RC=8, base=256,
-                   If=256, EE=64, GI=16))
-SCRATCH.update(_sb("int32", TB=[2, 6, 16], SN=42, i1=42, i2=42, P=8))
+SCRATCH.update(_sb("bfloat16", O=W, O2=M, YO=M + TR, DM=M, come0=16 + S, come1=16 + S, give0=S, give1=S, WB=W, U=W,
+                   same=192, s0=192, s2=192, cc=256, cl=240, ones=64, fl=192, dhi=192, LS=[len(LISTS), 240],
+                   Ib=128 * len(SCALES), Bs=144, Bh=144, Bl=144))
+SCRATCH.update(_sb("float16", PG=192, N1=192, N2=192, TS=192))
+SCRATCH.update(_sb("float32", SD=M, SL=W, TF=[6, 2, 16], TW=192, f2=42, LOC=240, sm=192, Z=768, ZM=256, col=16, RD=256, RG=32, RB=256,
+                   If=128, EE=64, GI=64))
+SCRATCH.update(_sb("int32", TB=[2, 6, 16], SN=42, i1=42, P=8))
 SCRATCH.update(_sb("uint16", dl=192, yl=192, xl=192, el=WC, sl=42, pl=64))
-PSUM = ("A0", "A1", "G0", "G1", "G2", "KK", "AB", "PT")
+PSUM = ("A0", "A1", "G0", "G1", "G2", "KK", "S0", "S1")
 for _n in PSUM:
     SCRATCH[_n] = ("psum", [128, 512], "float32")
 NDMA = 40
 SEMAPHORES = ["cv", "ca", "cp", "cg", "arr0", "arr1", "snt0", "snt1"] + ["d%d" % _k for _k in range(NDMA)]
-PLAN = {"yact": ((2, 3, 4, 5), (3, 4, 5)), "dact": ((), (5,)), "dchunk": 512, "xchunk": 512, "ychunk": 512, "tchunk": 512, "wchunk": 512,
-        "load": 1024, "ochunk": (1024, 512), "rem": (9.0, 7.5), "f": 1.0, "gat": 1.56, "row": 0.035, "dma": 1.7}
-ORDER = ("0M4G1n1s1x4L1i1H0R4w1M2Q393e1C2B2r2w2V2G2c112Z3o3y3S553j3D3X1d423I3t512h0j0o868a8g8k0e5Y0t8v6y684B344Q6i8F8J0W1W3N8q8z2m2L94988U8Y094c5p47045k5E5J5z5T5O5u8P9e21634h0y9r9x9h9nah6H0D0I9L9R165j5e9B9H279Va1a5ab6M7U837g4m1R6d7K7TalapaBaFaJ6T777c7lb06Xawb4b96n4raVbkaObdbnbsbxbC6s724W7Hc6c17s7x7CbMbT6FdXe8cseeenetbWcKcFbLcVcQehe2ewcdcicxcCdaded1djdtdodCdIdDdNf5d6fpeCeIffeLcnfaeReXf0fGfJgNg5fkfugHfQfVfYfzhbh1gagfgigsgndWhrhxhAgxgCgXkrhahhhpkBiSj0kvkQithKi9kFkLl0kUiziFiIhGhRhUl4lpmggVlClfi5igijlMlaltljlzi0iOipj2jBj7jejNmrmxlSmmlImHk6kekgkom6mclWm2n1mBnqmL1bpEpzjsjxjGpJjijnmQmWnen5nanlnunznKnDnNnXo2nSobjSjXock2oworp5ojomq4qaqdpPpVpYoDoSoXoIoNpfqjpaqpqsplprqyqCp2qWrbqHrnrqqRrKrTr6pwqMr1sJsRszsHrxrCrFt3rgtmtvtbtdtlrWs1s6sjs9sesostuluaujuttwtFtHtPu0u9tRtZsSt1")
+PLAN = {"yact": ((2, 3, 4, 5), (3, 4, 5)), "dact": ((), ()), "dchunk": 512, "xchunk": 512, "ychunk": 512, "tchunk": 512, "wchunk": 512,
+        "ochunk": 1024, "rem": (2.7, 1.0), "remrows": 3.8, "gat": 1.56, "row": 0.02, "dma": 0.8, "wake": 0.06,
+        "tries": 220000, "seed": 1, "mean": 0.05, "heat": 0.15, "share": 1.0, "fill": 2048, "lean": 0.3, "apart": True, "give": ("v", "av"),
+        "load": ((0, 2048), (2048, 3072)),
+        "due": {"give": (3.0, 19.0, 0, 0), "digits": (2.0, 22.5, 0, 0), "slots": (9.0, 26.0, 0, 0), "rows": (8.0, 25.0, 0, 0),
+                "same": (3.0, 24.0, 0, 0), "next": (3.2, 27.0, 0, 0), "prev": (12.6, 28.6, 0, 0), "edge": (3.5, 19.5, 0.5, 0.7),
+                "twin": (5.0, 21.0, 0.7, 0.7), "key": (8.0, 24.0, 1.5, 1.5), "pos": (13.5, 29.5, 0, 0), "border": (13.0, 29.0, 0, 0),
+                "flips": (12.5, 28.5, 0, 0), "lists": (16.0, 32.0, 0, 0), "corners": (17.0, 33.0, 0.2, 0.2), "sends": (16.5, 0, 0, 0),
+                "twins": (18.5, 35.0, 1.0, 0)}}
+
+
+DEALT = []
 
 
 def meet(x, y):
@@ -39,7 +52,6 @@ def meet(x, y):
 def link(ops):
     touch = {}
     for n, o in enumerate(ops):
-        o["id"] = n
         o["banks"] = set(r[0] for r in o["r"] + o["w"] if r[0] in PSUM)
         near = set()
         for r in o["r"] + o["w"]:
@@ -56,13 +68,186 @@ def link(ops):
             touch.setdefault(r[0], set()).add(n)
 
 
+def place(ops, pre, rank, plan, back, only):
+    busy = {e: [] for e in "vapgsd"}
+    left = [len(p) for p in pre]
+    after = [[] for _ in ops]
+    for n, p in enumerate(pre):
+        for m in p:
+            after[m].append(n)
+    begin, done, at = {}, {}, {}
+    ready = [n for n in range(len(ops)) if not left[n]]
+
+    def gap(e, t, c):
+        for a, b in busy[e]:
+            if t + c <= a:
+                break
+            t = max(t, b)
+        return t
+
+    while ready:
+        n = min(ready, key=lambda n: (rank[n], n))
+        ready.remove(n)
+        o = ops[n]
+        best = None
+        for e in only.get(n, o["alt"]):
+            t = max([0.0] + [done[m] + (0.0 if at[m] == e == "p" else plan["wake"]) for m in pre[n]]) + (o["lat"] if back else 0.0)
+            use = [(e, o["c"])] if o["kind"] == "c" else [(e, 0.05), ("d", o["c"])]
+            if o["kind"] == "rem" and plan["apart"]:
+                use = [(e, 0.3)]
+            while True:
+                u = max(gap(x, t, c) for x, c in use)
+                if u == t:
+                    break
+                t = u
+            t2 = t + (plan["lean"] if e == "v" and len(o["alt"]) > 1 else 0.0)
+            if best is None or t2 < best[0]:
+                best = (t2, t, e, use)
+        _, t, e, use = best
+        for x, c in use:
+            busy[x].append((t, t + c))
+            busy[x].sort()
+        begin[n], done[n], at[n] = t, t + o["c"] + (0.0 if back else o["lat"]), e
+        for m in after[n]:
+            left[m] -= 1
+            if not left[m]:
+                ready.append(m)
+    return begin, done, at
+
+
+def deal(ops, plan):
+    pre, above = [], []
+    for o in ops:
+        p = [m for m, _ in o["pre"]]
+        far = set().union(*(above[m] for m in p))
+        pre.append([m for m in p if m not in far])
+        above.append(far.union(p))
+    post = [[] for _ in ops]
+    rank = [o["due"] for o in ops]
+    for n in reversed(range(len(ops))):
+        for m in pre[n]:
+            rank[m] = min(rank[m], rank[n] - 1e-6)
+            post[m].append(n)
+    best = None
+    for _ in range(plan["passes"]):
+        begin, done, at = place(ops, pre, rank, plan, False, {})
+        worth = max(done.values()) + plan["mean"] * sum(done.values()) / len(ops)
+        if best is None or worth < best[0]:
+            best = (worth, begin, at, rank, {})
+        _, done, _ = place(ops, post, [-done[n] for n in range(len(ops))], plan, True, {})
+        rank = [-done[n] for n in range(len(ops))]
+    seed = plan["seed"]
+    now = best
+    for i in range(plan["tries"]):
+        rank, only = [now[1][n] for n in range(len(ops))], dict(now[4])
+        seed = (seed * 1103515245 + 12345) % 2 ** 31
+        n, k = seed // 64 % len(ops), seed // 2 ** 20 % 16
+        if len(ops[n]["alt"]) > 1 and k < 6:
+            only[n] = ("a", "v", "av")[k % 3]
+        else:
+            new = rank[n] + (k - 9.5) * abs(k - 9.5) * plan["jump"]
+            for m in above[n]:
+                rank[m] = min(rank[m], new - 1e-3 * (rank[n] - rank[m]))
+            rank[n] = new
+        begin, done, at = place(ops, pre, rank, plan, False, only)
+        worth = max(done.values()) + plan["mean"] * sum(done.values()) / len(ops)
+        if worth <= now[0] + plan["heat"] * (1 - i / plan["tries"]) * (seed // 2 ** 24 % 8) / 8:
+            now = (worth, begin, at, rank, only)
+            if worth < best[0]:
+                best = now
+    return [(n, best[2][n]) for n in sorted(best[1], key=lambda n: (best[1][n], n))]
+
+
+def play(ops, pre, order, at, plan):
+    free = {e: 0.0 for e in "vapgsd"}
+    last, done, by = {}, {}, {}
+    wake = plan["wake"]
+    for n in order:
+        o, e = ops[n], at[n]
+        t, x, held = free[e], last.get(e), True
+        for m in pre[n]:
+            u = done[m] if e == "p" == at[m] else done[m] + wake
+            if u > t:
+                t, x, held = u, m, False
+        if o["kind"] == "c":
+            done[n] = free[e] = t + o["c"]
+        else:
+            free[e] = t + o["hold"]
+            if free["d"] > t + o["lat"] / 2:
+                t, x, held = free["d"] - o["lat"] / 2, last["d"], True
+            free["d"] = t + o["lat"] / 2 + o["c"] * (plan["share"] if o["kind"] == "rem" else 1)
+            done[n] = t + o["lat"] + o["c"]
+            last["d"] = n
+        last[e] = n
+        by[n] = (x, held)
+    n = max(done, key=done.get)
+    worth, path = done[n] + plan["mean"] * sum(done.values()) / len(done), []
+    while n is not None:
+        path.append((n, by[n][0] if by[n][1] else None))
+        n = by[n][0]
+    return worth, path
+
+
+def deal(ops, plan):
+    pre, above = [], []
+    for o in ops:
+        p = [m for m, _ in o["pre"]]
+        far = set().union(*(above[m] for m in p))
+        pre.append([m for m in p if m not in far])
+        above.append(far.union(p))
+    rank = [o["due"] for o in ops]
+    for n in reversed(range(len(ops))):
+        for m in pre[n]:
+            rank[m] = min(rank[m], rank[n] - 1e-6)
+    order = sorted(range(len(ops)), key=lambda n: rank[n])
+    at = {n: o["alt"][0] for n, o in enumerate(ops)}
+    now = play(ops, pre, order, at, plan)
+    best = (now[0], order, at)
+    seed = [plan["seed"]]
+
+    def draw(k):
+        seed[0] = (seed[0] * 1103515245 + 12345) % 2 ** 31
+        return seed[0] // 256 % k
+
+    for i in range(plan["tries"]):
+        n, m = now[1][draw(len(now[1]))]
+        k = draw(16)
+        o2, a2 = order, at
+        if k < 3:
+            n = draw(len(ops))
+            same = [x for x in order[:order.index(n)] if at[x] == at[n]]
+            m = same[-1] if same else None
+        if len(ops[n]["alt"]) > 1 and k % 4 == 0:
+            a2 = dict(at)
+            a2[n] = "a" if at[n] == "v" else "v"
+            if k >= 8:
+                b = order.index(n)
+                near = [x for x in order[max(0, b - 25):b + 25] if len(ops[x]["alt"]) > 1 and at[x] == a2[n]]
+                if near:
+                    a2[near[draw(len(near))]] = at[n]
+        elif m is None or m in above[n]:
+            continue
+        else:
+            a, b = order.index(m), order.index(n)
+            if k % 2:
+                first = [x == n or x in above[n] for x in order[a:b + 1]]
+            else:
+                first = [not (x == m or m in above[x]) for x in order[a:b + 1]]
+            o2 = (order[:a] + [x for x, f in zip(order[a:b + 1], first) if f] + [x for x, f in zip(order[a:b + 1], first) if not f]
+                  + order[b + 1:])
+        new = play(ops, pre, o2, a2, plan)
+        if new[0] <= now[0] + plan["heat"] * (1 - i / plan["tries"]) * draw(8) / 8:
+            now, order, at = new, o2, a2
+            if now[0] < best[0]:
+                best = (now[0], order, at)
+    return [(n, best[2][n]) for n in best[1]]
+
+
 def emit(g, T, ops, order):
     q = {"v": g.vector, "a": g.scalar, "p": g.tensor, "g": g, "s": g.sync}
     know = {e: ({}, set()) for e in q}
-    assert sorted(m for m, _ in order) == list(range(len(ops)))
     for n, (m, e) in enumerate(order):
         o = ops[m]; o["e"] = e; o["n"] = n; deps = []
-        assert e in o["alt"] and all("n" in ops[x] for x, _ in o["pre"])
         for x, raw in o["pre"]:
             d = ops[x]
             if d["kind"] == "rem" or (d["kind"] == "c" and o["kind"] == "c" and d["e"] == e and (e == "p" or not raw)):
@@ -105,9 +290,15 @@ def emit(g, T, ops, order):
 
 def calls(core, rank, T, topo, plan):
     ops = []
+    now = [0.0]
+
+    def due(t):
+        now[0] = t
 
     def R(name, lo, hi, step=1, row=None):
         part = slice(0, 128) if row is None else slice(row, 128, 16)
+        if name in LISTS:
+            return (T.LS[:, LISTS.index(name), lo:hi], [(name, lo, hi, None)], hi - lo, 2)
         ap = T[name][part, lo:hi] if step == 1 else T[name][part, lo:hi:step]
         return (ap, [(name, lo, hi, row)], len(range(lo, hi, step)), 4 if SCRATCH[name][2].endswith("32") else 2)
 
@@ -115,10 +306,11 @@ def calls(core, rank, T, topo, plan):
         return (win[0].indirect(off[0]), win[1] + off[1], 16 * off[2], 0)
 
     def add(e, kind, fn, w, r, c, lat=0.0, ext=()):
-        ops.append({"e": e[0], "alt": e, "kind": kind, "fn": fn, "w": list(w), "r": list(r), "ext": list(ext), "c": c, "lat": lat})
+        ops.append({"alt": e, "kind": kind, "fn": fn, "w": list(w), "r": list(r), "ext": list(ext), "c": c, "lat": lat,
+                    "due": now[0] + 1e-4 * len(ops), "hold": 0.05 if kind == "dma" else lat - 0.7})
 
     def cost(out, a, cycles=1.0):
-        return 0.05 + 0.83e-3 * plan["f"] * (plan["gat"] * a[2] if a[3] == 0 else max(64, out[2] * cycles))
+        return 0.055 + 0.83e-3 * (plan["gat"] * a[2] if a[3] == 0 else max(64, out[2] * cycles))
 
     def tt(out, a, b, op, ext=()):
         both = a[1][0][0] not in PSUM and b[1][0][0] not in PSUM
@@ -131,14 +323,15 @@ def calls(core, rank, T, topo, plan):
                 r += s[1]; v.append(s[0])
             else:
                 v.append(s)
+        c = cost(out, a, 0.5 if out[3] == a[3] == 2 else 1)
         if op1 is None:
-            add("v", "c", lambda q, e: q.tensor_scalar(out[0], a[0], v[0], None, op0), out[1], r, cost(out, a))
+            add("v", "c", lambda q, e: q.tensor_scalar(out[0], a[0], v[0], None, op0), out[1], r, c)
         else:
-            add("v", "c", lambda q, e: q.tensor_scalar(out[0], a[0], v[0], v[1], op0, op1), out[1], r, cost(out, a))
+            add("v", "c", lambda q, e: q.tensor_scalar(out[0], a[0], v[0], v[1], op0, op1), out[1], r, c)
 
     def cp(out, a, e="v", ext=()):
         add(e, "c", lambda q, e: q.tensor_copy(out[0], a[0]) if e == "v" else q.activation(out[0], a[0], F.Copy), out[1], a[1],
-            cost(out, a, 0.5 if e == "v" and out[3] == a[3] == 2 else 1), 0.0, ext)
+            cost(out, a), 0.0, ext)
 
     def act(out, a, func, scale=1.0, bias=None):
         if bias is None:
@@ -146,9 +339,10 @@ def calls(core, rank, T, topo, plan):
         else:
             add("a", "c", lambda q, e: q.activation(out[0], a[0], func, bias=bias, scale=scale), out[1], a[1], cost(out, a))
 
-    def scale(out, a, c):
-        add("av", "c", lambda q, e: q.tensor_scalar(out[0], a[0], c[0], None, A.mult) if e == "v"
-            else q.activation(out[0], a[0], F.Copy, scale=c[0]), out[1], a[1] + c[1], cost(out, a))
+    def affine(out, a, mul, plus):
+        b, r = (plus[0], plus[1]) if isinstance(plus, tuple) else (plus, [])
+        add("av", "c", lambda q, e: q.tensor_scalar(out[0], a[0], mul, b, A.mult, A.add) if e == "v"
+            else q.activation(out[0], a[0], F.Identity, bias=b, scale=mul), out[1], a[1] + r, cost(out, a))
 
     def group(out, terms, start=True, stop=True):
         def fn(q, e):
@@ -156,7 +350,7 @@ def calls(core, rank, T, topo, plan):
                 ins = q.matmul((t[2] if len(t) > 2 else out)[0], t[0][0], t[1][0], start and k == 0, stop and k == len(terms) - 1)
             return ins
         add("p", "c", fn, out[1], sum((t[0][1] + t[1][1] for t in terms), []),
-            sum(0.417e-3 * plan["f"] * max(64, t[1][2]) * (4 if t[0][3] == 4 else 1) for t in terms))
+            sum(0.417e-3 * max(64, t[1][2]) * (4 if t[0][3] == 4 else 1) for t in terms))
 
     def ms(out, c):
         add("v", "c", lambda q, e: q.memset(out[0], c), out[1], [], cost(out, out, out[3] / 4))
@@ -168,85 +362,79 @@ def calls(core, rank, T, topo, plan):
         else:
             add("g", "c", lambda q, e: q.iota(out[0], pat, base, cm), out[1], [], c)
 
-    def dma(out, a, row):
-        add("s", "dma", lambda q, e: q.dma_start(out[0], a[0]), out[1], a[1], 8 * (plan["row"] + row / 22e3), plan["dma"])
+    def dma(out, a, row, rows=8):
+        add("s", "dma", lambda q, e: q.dma_start(out[0], a[0]), out[1], a[1], rows * (plan["row"] + row / 22e3), plan["dma"])
 
-    def side(name, p, n=64):
-        return R(name, p * n, (p + 1) * n)
+    def side(name, p, n=64, at=0):
+        return R(name, at + (p % 3) * n, at + (p % 3 + 1) * n)
 
     def chunks(step, skip):
         out = []
-        for k in range(6):
-            if k not in skip:
-                if out and out[-1][1] == 512 * k and out[-1][1] % step:
+        for lo in range(0, M, min(step, 512)):
+            if lo // 512 not in skip:
+                if out and out[-1][1] == lo and lo % step:
                     out[-1][1] += 512
                 else:
-                    out.append([512 * k, 512 * k + 512])
+                    out.append([lo, lo + min(step, 512)])
         return out
 
     col = lambda k: R("col", k, k + 1)
     Ib = lambda k: R("Ib", 128 * k, 128 * k + 128)
-    I1, IN, NB, I1536, K1, KN, I219, IW, I16, ZERO = (Ib(k) for k in range(10))
-    IF, IFN = (R("If", 128 * k, 128 * k + 128) for k in range(2))
+    I1, IN, ZERO, IW, I16, K1, KN, K3, N192 = (Ib(k) for k in range(len(SCALES)))
+    IF = R("If", 0, 128)
 
     for gl in range(2):
         dma((T.TB[:, gl], [("TB", gl, gl + 1, None)]), (T.twn[gl:8:2, :], []), 384)
     dma(R("SN", 0, 42), (T.snd[:, :], []), 168)
-    for lo, hi in chunks(plan["load"], ()):
+    for lo, hi in plan["load"]:
         dma(R("O", (lo + TR) % M, (lo + TR) % M + hi - lo), (T.x[:, lo:hi], []), 2 * (hi - lo))
     for p in range(3):
-        dma(side("O2", p, TR), (T.x[:, ((p + 2) % 3) * TR:((p + 2) % 3 + 1) * TR], []), 2048)
+        dma(side("O2", p, TR), (T.x[:, (p + 2) % 3 * TR:((p + 2) % 3 + 1) * TR], []), 2 * TR)
 
     iota(R("P", 0, 1), [[0, 1]], 0, 1, small=False)
     iota(R("RD", 0, 256), [[1, 256]])
-    iota(R("RC", 0, 8), [[1, 8]])
-    iota(R("ones", 0, 192), [[0, 192]], 1)
-    iota(R("WB", 2048, W), [[0, W - 2048]])
+    iota(R("RG", 0, 8 * DUP), [[1, 8], [0, DUP]])
+    iota(R("RB", 0, 64 * DUP), [[0, 4 * DUP], [1, DUP], [0, 16 // DUP]])
+    iota(R("cc", 0, 256), [[16, 256]])
+    iota(R("ones", 0, 64), [[0, 64]], 1)
+    iota(R("WB", 0, plan["fill"]), [[0, plan["fill"]]])
+    due(6.0)
+    iota(R("WB", plan["fill"], W), [[0, W - plan["fill"]]])
+    for r in range(2):
+        iota(R("come%d" % r, 0, 16), [[0, 16]], -256)
     iota(R("SL", M, W), [[0, S]])
-    ms(R("O", M, W), 0.0)
-    ts(R("P", 1, 2), R("P", 0, 1), 1, A.bitwise_and)
-    ts(R("P", 2, 3), R("P", 0, 1), 1, A.arith_shift_right)
+    due(1.0)
+    ms(R("O", M, W), FAR)
+    ts(R("P", 1, 2), R("P", 0, 1), DUP - 1, A.bitwise_and)
+    ts(R("P", 2, 3), R("P", 0, 1), DUP // 2, A.arith_shift_right)
     ts(R("P", 3, 4), R("P", 0, 1), 4, A.arith_shift_right)
     ts(R("P", 4, 5), R("P", 0, 1), 15, A.bitwise_and)
-    ms(ZERO, 0.0)
     cp(R("col", 0, 5), R("P", 0, 5))
     ts(IF, R("RD", 0, 128), col(0), A.is_equal)
-    ts(R("base", 0, 256), R("RD", 0, 256), 16.0, A.mult, col(4), A.add)
-    ts(R("GI", 0, 8), R("RC", 0, 8), col(3), A.is_equal)
-    ts(R("GI", 8, 16), R("RC", 0, 8), col(3), A.is_equal, -1.0, A.mult)
-    act(IFN, IF, F.Copy, -1.0)
     for n, s in enumerate(SCALES):
-        act(Ib(n), IF, F.Copy, s)
-    act(R("c16", 0, 256), R("RD", 0, 256), F.Copy, 16.0)
-    ts(R("cl", 0, 192), R("ones", 0, 192), col(4), A.mult, 7.5, A.subtract)
-    ts(col(8), col(1), 0.0, A.is_equal)
-    ts(R("EE", 0, 64), R("RD", 0, 64), col(2), A.is_equal, 4.0, A.mult)
-    ts(col(5), col(3), 16.0, A.mult, 15.0, A.add)
+        affine(Ib(n), IF, s, 0.0)
+    ts(R("GI", 0, 8 * DUP), R("RG", 0, 8 * DUP), col(3), A.is_equal)
+    affine(R("GI", 32, 32 + 8 * DUP), R("GI", 0, 8 * DUP), -1.0, 0.0)
+    affine(col(9), col(4), 1.0, -7.5)
+    affine(R("cl", 0, 240), R("RD", 0, 240), 0.0, col(9))
+    due(3.0)
+    ts(R("ZM", 0, 64 * DUP), R("RB", 0, 64 * DUP), col(1), A.is_equal)
+    ts(R("EE", 0, 128 // DUP), R("RD", 0, 128 // DUP), col(2), A.is_equal, 4.0, A.mult)
+    add("v", "c", lambda q, e: q.memset(T.LS[:, :, 192:240], 0.0), [(nm, 192, 240, None) for nm in LISTS], [], 0.155)
+    affine(col(5), col(3), 16.0, 15.0)
     ts(col(6), col(4), 0.0, A.is_equal)
     ts(col(7), col(4), 1.0, A.is_equal, float(WC), A.mult)
-    ts(col(9), col(4), 2.0, A.is_equal, 1.0 / 16, A.mult)
-    ms(R("WB", 0, 1024), 0.0)
-    ms(R("WB", 1024, 2048), 0.0)
-    ts(R("Bs", 0, 144), R("RD", 0, 144), col(5), A.is_equal, col(6), A.mult)
-    tt(col(7), col(7), col(9), A.add)
-    ts(R("ci", 0, 64), R("ones", 0, 64), col(4), A.mult)
-    ms(R("b16", 256, 304), 0.0)
-    ms(R("low", 256, 304), 0.0)
-    ts(R("Bh", 0, 144), R("RD", 0, 144), col(5), A.is_equal, col(7), A.mult)
-    ts(col(10), col(4), 2.5, A.subtract)
-    tt(col(10), col(10), col(10), A.mult)
-    ts(col(10), col(10), 3.0, A.is_lt)
-    ts(R("Bl", 0, 144), R("RD", 0, 144), col(5), A.is_equal, col(10), A.mult)
-    for r in range(2):
-        ms(R("come%d" % r, 0, 16), -256.0)
-    for nm in ("sel", "hi", "lo"):
-        ms(R(nm, 192, WC), 0.0)
-    cp(R("LOC", 192, WC), R("base", 192, WC), "a")
-    cp(R("hi2", 0, WC), R("c16", 0, WC), "av")
-    ts(R("lo2", 0, WC), R("RD", 0, WC), 0.0, A.mult, R("cl", 0, 1), A.add)
-    dma(R("WB", 0, W, row=3), R("hi2", 0, WC), 468)
-    dma(R("WB", 0, W, row=4), R("lo2", 0, WC), 468)
+    ts(col(8), col(4), 2.0, A.is_equal, 1.0 / 16, A.mult)
+    affine(col(7), col(8), 1.0, col(7))
+    ts(col(10), col(4), 2.5, A.is_gt)
+    for nm, k in (("Bs", 6), ("Bh", 7), ("Bl", 10)):
+        ts(R(nm, 0, 144), R("RD", 0, 144), col(5), A.is_equal, col(k), A.mult)
+    due(7.0)
+    affine(R("LOC", 192, 240), R("RD", 192, 240), 16.0, col(4))
+    dma(R("WB", 0, W, row=3), R("cc", 0, WC), 468)
+    dma(R("WB", 0, W, row=4), R("cl", 0, WC), 468)
 
+    due(0.5)
     for gl in range(2):
         add("v", "c", lambda q, e, gl=gl: q.tensor_scalar(T.TF[:, :, gl, :], T.TB[:, gl], -7.5, None, A.add),
             [("TF", 0, 2, gl)], [("TB", gl, gl + 1, None)], 0.13)
@@ -254,35 +442,43 @@ def calls(core, rank, T, topo, plan):
         add("v", "c", lambda q, e, b=b: q.transpose(T.TW[:, b:192:6], T.TF[:, b]), [("TW", 0, 192, b)], [("TF", 0, 2, None)], 0.11)
     cp(R("sl", 0, 42), R("SN", 0, 42))
     ts(R("dl", 0, 192), R("TW", 0, 192), 7.5, A.add)
+    due(8.0)
     ts(R("i1", 0, 42), R("SN", 0, 42), 15, A.bitwise_and)
-    ts(R("i2", 0, 42), R("SN", 0, 42), 4, A.arith_shift_right)
-    ts(R("f2", 0, 42), R("i1", 0, 42), float(WC), A.mult)
-    tt(R("f2", 0, 42), R("f2", 0, 42), R("i2", 0, 42), A.add)
-    cp(R("el", 0, 42), R("f2", 0, 42))
+    ts(R("f2", 0, 42), R("i1", 0, 42), 16.0 * WC - 1, A.mult)
+    tt(R("f2", 0, 42), R("f2", 0, 42), R("SN", 0, 42), A.add)
+    ts(R("el", 0, 42), R("f2", 0, 42), 1.0 / 16, A.mult)
 
-    TW = R("TW", 0, 192)
-    BB, AA = R("AB", 0, 192), R("AB", 192, 384)
-    k = lambda p: R(("A0", "A1", "KK")[p], 0, 64)
-    sel = lambda p: side("sel", p)
+    PHI, TN = R("KK", 0, 64), R("G2", 320, 384)
+    key = lambda p: R("G%d" % p, 256, 320)
+    own = lambda q: [(I1, side("cc", q)), (I1, R("cl", 0, 64))]
+    far = lambda q: [(I1, side("dlo", q)), (I1, side("dhi", q))]
+    times = lambda k, a: [(K1 if k > 0 else KN, a)] * abs(k)
     stage = [0]
 
     def staging():
         stage[0] += 1
-        return R("A%d" % (1 - stage[0] % 2), 0, 512)
+        return "A%d" % (1 - stage[0] % 2)
 
     def reduce(p, first):
-        nm = "SL" if first else "SD"
-        terms = [(R(nm, p * TR + j, (p + 1) * TR, 8), R("GI", 0, 8) if first else R("GI", 8, 16), R("G%d" % p, j, 64, 8)) for j in range(8)]
-        group(R("G%d" % p, 0, 64), ([(ZERO, R("ones", 0, 64))] if first else []) + terms, first, not first)
+        nm, gi, n, step = ("SL", 0) if first else ("SD", 32), None, 2 * TR // DUP, 16 // DUP
+        for h in range(DUP // 2):
+            terms = [(R(nm[0], p * TR + h * n + j, p * TR + h * n + n, step), R("GI", nm[1], nm[1] + 8 * DUP),
+                      R("G%d" % p, 128 * h + j, 128 * h + 128, step)) for j in range(step)]
+            start = first and h == 0
+            group(R("G%d" % p, 0, 64 * DUP), ([(ZERO, R("cc", 0, 64 * DUP))] if start else []) + terms, start,
+                  not first and h == DUP // 2 - 1)
 
-    def compact(out, B, lo, hi, more=()):
-        group(out, list(more) + [(R(B, 15 - i, 143 - i), R("U", lo + i, hi, 16)) for i in range(16)])
+    def compact(out, B, lo, hi):
+        group(out, [(R(B, 15 - i, 143 - i), R("U", lo + i, hi, 16)) for i in range(16)])
 
     for r in range(2):
+        TW = R("TW", 0, 192) if r == 0 else R("KK", 128, 320)
         come = R("come%d" % r, 0, 16 + S)
         come = (come[0], come[1] + [("arr%d" % r, 0, 1, None)], come[2], come[3])
         arr = [("arr%d" % r, N - 1)]
-        cp(R("give%d" % r, 0, S), ind(R("O", 0, M), R("sl", 0, 42)), "av")
+        when = lambda step, k=0, r=r: due(plan["due"][step][r] + k * plan["due"][step][2 + r])
+        when("give")
+        cp(R("give%d" % r, 0, S), ind(R("O", 0, M), R("sl", 0, 42)), plan["give"][r])
         trs = []
         for d in range(1, N):
             dst = T.cores[(rank + d) % N]
@@ -291,131 +487,136 @@ def calls(core, rank, T, topo, plan):
                                          remote_sem=T.sem["arr%d" % r], src=T["give%d" % r][:, (d - 1) * C:d * C],
                                          dst=T["come%d" % r][:, 16 + (d - 1) * C:16 + d * C]))
         add("g", "rem", lambda q, e, trs=trs, r=r: q.remote_dma_fused(trs, local_sem=T.sem["snt%d" % r]), [("arr%d" % r, 0, 1, None)],
-            [("give%d" % r, 0, S, None)], 0.3, plan["rem"][r])
+            [("give%d" % r, 0, S, None)], plan["remrows"], plan["rem"][r])
+        when("digits")
         ts(R("b16", 0, 192), TW, R16, A.add, R16, A.subtract)
         tt(R("low", 0, 192), TW, R("b16", 0, 192), A.subtract)
-        less = [(I1, R("b16", 0, 192)), (I1, R("low", 0, 192)), (IN, R("c16", 64, 256)), (IN, R("cl", 0, 192))]
-        group(BB, less)
-        act(R("bord", 0, 192), TW, F.Relu, 1.0, 8.5 - M)
-        act(R("sgn", 0, 192), TW, F.Sign, -1.0, TR - 8.0)
-        act(R("f1", 0, 192), BB, F.Identity, 1.0, R1K)
-        act(R("f1", 0, 192), R("f1", 0, 192), F.Identity, 1.0, -R1K)
+        ts(R("s0", 0, 192), R("b16", 0, 192), TR - 8.0, A.is_lt)
+        ts(R("s2", 0, 192), R("b16", 0, 192), 2 * TR - 8.0, A.is_gt)
+        when("slots")
         ts(R("yl", 0, 192), TW, 23.5 - M, A.add, 15.0, A.max)
-        tt(R("same", 0, 192), BB, R("f1", 0, 192), A.is_equal)
-        for lo, a, b in ((64, 0, 192), (0, 128, 192), (256, 0, 64)):
-            group(R("PT", lo, lo + b - a), [(IW, R("low", a, b)), (I16, R("b16", a, b)),
-                                            (I1536, R("ones", a, b)), (I219, R("ones", a, b))])
-        group(AA, less + [(I1536, R("sgn", 0, 192)), (I1536, R("ones", 0, 192))])
+        when("rows")
         for row, nm in ((1, "low"), (2, "b16")):
-            cp(R(nm, 192, 256), R(nm, 0, 64), "av")
-            dma(R("WB", 0, W, row=row), R(nm, 64, 64 + WC), 468)
+            dma(R("WB", 0, W, row=row), R(nm, 0, WC), 468)
+        when("same")
+        for p in range(3):
+            group(side("KK", p, at=320), own(1) + [(IN, side("b16", p)), (IN, side("low", p)), (KN, side("s0", p)), (K1, side("s2", p))])
+        ts(R("same", 0, 192), R("KK", 320, 512), 0.0, A.is_equal, -BIG, A.mult)
+        when("next")
+        for q in range(3):
+            group(side("S0", q, at=256), [(IW, side("low", q - 1)), (I16, side("b16", q - 1)), (N192, side("s2", q - 1))])
+        when("prev")
+        for q in range(3):
+            group(side("S1", q), [(I1, side("low", q - 1)), (IN, R("cl", 0, 64))])
+            group(side("S1", q, at=192), [(I1, side("b16", q - 1)), (K3, side("s0", q - 1)), (IN, R("cc", 64 * q + 64, 64 * q + 128))])
         for p in range(3):
             for h in range(2):
-                s = staging()
-                group(s, [(I1, side("O", 2 * ((p + 1) % 3) + h, 512)), (IN, side("O", 2 * ((p + 2) % 3) + h, 512))])
-                act(side("SL", 2 * p + h, 512), s, F.Square)
+                when("edge", 2 * p + h)
+                s = R(staging(), 0, 512)
+                group(s, [(I1, R("O", (p + 1) % 3 * TR + 512 * h, (p + 1) % 3 * TR + 512 * h + 512)),
+                          (IN, R("O", (p + 2) % 3 * TR + 512 * h, (p + 2) % 3 * TR + 512 * h + 512))])
+                act(R("SL", p * TR + 512 * h, p * TR + 512 * h + 512), s, F.Square)
             reduce(p, True)
         for lo, hi in chunks(plan["dchunk"], plan["dact"][r]):
+            when("twin", lo / 512)
             tt(R("SD", lo, hi), ind(R("O", 0, W), R("dl", lo // 16, hi // 16)), R("O2", lo, hi), A.subtract)
             act(R("SD", lo, hi), R("SD", lo, hi), F.Square)
         for n in plan["dact"][r]:
-            cp(side("DM", n, 512), ind(R("O", 0, W), side("dl", n, 32)), "a")
-            s = staging()
-            group(s, [(I1, side("DM", n, 512)), (IN, side("O", n, 512))])
-            act(side("SD", n, 512), s, F.Square)
+            lo, hi = 512 * n, 512 * n + 512
+            cp(R("DM", lo, hi), ind(R("O", 0, W), R("dl", lo // 16, hi // 16)), "a")
+            s = R(staging(), 0, 512)
+            group(s, [(I1, R("DM", lo, hi)), (IN, R("O", lo, hi))])
+            act(R("SD", lo, hi), s, F.Square)
         for p in range(3):
+            when("key", p)
             reduce(p, False)
-            for b in range(2):
-                scale((T.Z[:, p, :, b, :], [("Z", p, p + 1, b)], 64, 4), R("G%d" % p, 0, 64), col((8, 1)[b]))
-            if p == 1:
-                ts(side("sm", 0), k(0), 3.0, A.max)
-            if p == 2:
-                tt(side("sm", 1), k(1), side("sm", 0), A.max)
-            group(k(p), [(NB, side("same", p)), (NB, side("bord", p))] + [(I1, side("ones", 0))] * (2 - p)
-                  + [((T.Z[:, p], [("Z", p, p + 1, None)], 128, 4), R("EE", 0, 64))])
-        tt(side("sm", 2), k(2), side("sm", 1), A.max)
+            tt(side("Z", p, 64 * DUP), R("G%d" % p, 0, 64 * DUP), R("ZM", 0, 64 * DUP), A.mult)
+            n = 128 // DUP
+            group(key(p), [(I1, side("same", p))] + [(IN, R("ones", 0, 64))] * (p + 1)
+                  + [(R("Z", 64 * DUP * p + 128 * h, 64 * DUP * p + 128 * h + 128), R("EE", 0, n), R("G%d" % p, 256 + h * n, 256 + h * n + n))
+                     for h in range(DUP // 2)])
+            if p == 0:
+                add("av", "c", lambda q, e: q.tensor_scalar(side("sm", 0)[0], key(0)[0], 0.0, None, A.max) if e == "v"
+                    else q.activation(side("sm", 0)[0], key(0)[0], F.Relu), side("sm", 0)[1], key(0)[1], 0.11)
+            else:
+                tt(side("sm", p), key(p), side("sm", p - 1), A.max)
         for p in range(3):
-            tt(sel(p), k(p), side("sm", 2), A.is_equal)
+            tt(side("sel", p + 1), key(p), side("sm", 2), A.is_equal)
         dma(R("WB", 0, W, row=0), R("sel", 0, WC), 468)
-        tt(R("PG", 0, 192), R("PT", 64, 256), R("sel", 0, 192), A.mult)
-        group(R("KK", 192, 256), [(IF, side("PG", p)) for p in range(3)])
-        cp(R("pl", 0, 64), R("KK", 192, 256))
-        tt(R("MA", 0, 192), AA, R("sel", 0, 192), A.mult)
-        tt(R("MB", 0, 192), BB, R("sel", 0, 192), A.mult)
-        MA = lambda p: (IF, side("MA", p))
-        MB = lambda p: (IF, side("MB", p))
-        group(side("G0", 0), [MA(0), MB(2)] + [(I1536, sel(2))] * 2 + [(K1, sel(1))])
-        group(side("G0", 1), [MA(1), MB(0), (K1, sel(2))])
-        group(side("G0", 2), [MA(2), MB(1)] + [(KN, sel(0))] * 2)
-        group(side("G1", 0), [MA(2)] + [(K1, sel(2)), (K1, sel(1))] * 2)
-        group(side("G1", 1), [MA(0), (KN, sel(0)), (KN, sel(2))])
-        group(side("G1", 2), [MA(1), (KN, sel(1)), (KN, sel(0))])
-        tt(R("N1", 0, 192), R("PT", 0, 192), R("sel", 0, 192), A.mult)
-        tt(R("N2", 0, 192), R("PT", 128, 320), R("sel", 0, 192), A.mult)
+        tt(R("PG", 0, 192), R("S0", 256, 448), R("sel", 0, 192), A.mult)
+        group(R("KK", 384, 448), [(I1, side("PG", p)) for p in range(3)])
+        ts(R("pl", 0, 64), R("KK", 384, 448), MID + 64, A.add)
         for h in range(2):
-            cp(side("U", h, 512), ind(R("WB", 0, W), side("pl", h, 32)), "av")
-        compact(R("KK", 256, 320), "Bs", 0, TR)
-        compact(R("AB", 384, 448), "Bh", 0, TR, [(I1536, R("ones", 0, 64)), (I219, R("ones", 0, 64))])
-        if r == 0:
-            cp(R("dh", 0, 192), R("G1", 0, 192), "av")
-            tt(R("dw", 0, 192), R("G1", 0, 192), R("dh", 0, 192), A.subtract)
-            for nm, src, row in (("hi", "dh", 1), ("lo", "dw", 2)):
-                for q in range(3):
-                    tt(side(nm, q), R("KK", 256, 320), side(src, q), A.mult)
-                dma(R("WB", 0, W, row=row), R(nm, 0, WC), 468)
+            cp(R("U", 512 * h, 512 * h + 512), ind(R("WB", 0, W), R("pl", 32 * h, 32 * h + 32)), "av")
+        compact(PHI, "Bs", 0, TR)
+        compact(TN, "Bh", 0, TR)
+        when("pos")
+        for k, p in enumerate((0, 1, 2, 0)):
+            group(R("S0", 64 * k, 64 * k + 64), [(IW, side("low", p)), (I16, side("b16", p))])
+        when("border")
         for lo, hi in chunks(plan["ychunk"], plan["yact"][r]):
             tt(R("YO", lo, hi), ind(come, R("yl", lo // 16, hi // 16)), R("O", lo, hi), A.max, arr)
         for n in plan["yact"][r]:
-            cp(side("DM", n, 512), ind(come, side("yl", n, 32)), "a", arr)
-            s = staging()
-            group(s, [(I1, side("DM", n, 512))])
-            tt(side("YO", n, 512), s, side("O", n, 512), A.max)
-        phi = R("phi", 0, 64)
-        cp(phi, R("KK", 256, 320), "av")
+            lo, hi = 512 * n, 512 * n + 512
+            cp(R("DM", lo, hi), ind(come, R("yl", lo // 16, hi // 16)), "a", arr)
+            s = R(staging(), 0, 512)
+            group(s, [(I1, R("DM", lo, hi))])
+            tt(R("YO", lo, hi), s, R("O", lo, hi), A.max)
+        dma(R("YO", M, M + TR), R("YO", 0, TR), 2 * TR)
+        fl = lambda q: side("fl", q)
+        when("flips")
         for q in range(3):
-            tt(side("XL", q), side("G0", q), phi, A.mult)
-            if r == 1:
-                tt(side("G1", q), side("G1", q), phi, A.mult)
-            tt(side("TS", q), R("AB", 384, 448), sel((q + 1) % 3), A.mult)
-        for lo, hi in ((0, 64), (64, 192)):
-            for a in range(lo, hi, 64):
-                group(R("A0", a, a + 64), [(I1, R("c16", a, a + 64)), (I1, R("ci", 0, 64)), (IF, R("XL", a, a + 64))])
-            cp(R("xl", lo, hi), R("A0", lo, hi))
-        if r == 1:
-            tt(R("LOC", 0, 192), R("G1", 0, 192), R("base", 0, 192), A.add)
+            tt(fl(q), PHI, side("sel", q), A.mult)
+        tt(R("dlo", 0, 192), R("S1", 0, 192), R("fl", 0, 192), A.mult)
+        tt(R("dhi", 0, 192), R("S1", 192, 384), R("fl", 0, 192), A.mult)
+        for q in range(3):
+            back = times(((q - 1) % 3 - q), fl(q - 1))
+            group(side("G1", q), [(I1, side("dhi", q))] + back if r == 0 else own(q) + far(q) + back)
+        if r == 0:
+            cp(R("hi", 0, 192), R("G1", 0, 192), "av")
+            dma(R("WB", 0, W, row=5), R("dlo", 0, WC), 468)
+            dma(R("WB", 0, W, row=6), R("hi", 0, WC), 468)
+        else:
+            affine(R("LOC", 0, 192), R("G1", 0, 192), 1.0, 7.5)
             dma(R("SL", 0, W, row=0), R("LOC", 0, WC), 936)
         for q in range(3):
-            group(side("G2", q), [(IF, side("N1", (q + 2) % 3)), (IFN, side("N2", (q + 2) % 3)), (IFN, side("N1", (q + 1) % 3)),
-                                  (IF, side("TS", q))])
+            group(side("G0", q), own(q) + far(q + 1) + times((q + 1) % 3 - q, fl(q + 1)) + far(q) + times(1, fl(q))
+                  + times((q + 1) % 3 - q, fl(q - 1)))
+        for lo, hi in ((0, 64), (64, 192)):
+            ts(R("xl", lo, hi), R("G0", lo, hi), 7.5, A.add)
+        when("lists")
+        tt(R("N1", 0, 192), R("S0", 64, 256), R("fl", 0, 192), A.mult)
+        tt(R("N2", 0, 192), R("S0", 0, 192), R("fl", 0, 192), A.mult)
         for q in range(3):
-            tt(side("EL", q), side("G2", q), phi, A.mult)
-        tt(R("EL", 0, 192), R("PT", 64, 256), R("EL", 0, 192), A.add)
-        cp(R("el", 42, WC), R("EL", 0, 192))
+            tt(side("TS", q), TN, fl(q), A.mult)
+        for q in range(3):
+            group(side("G2", q), [(IW, side("low", q)), (I16, side("b16", q)), (I1, side("N1", q)), (IN, side("N2", q)),
+                                  (IN, side("N1", q - 1)), (I1, side("TS", q - 1))])
+        ts(R("el", 42, WC), R("G2", 0, 192), MID, A.add)
         for lo, hi in chunks(plan["xchunk"], ()):
-            cp(R("O", lo, hi), ind(R("YO", 0, M), R("xl", lo // 16, hi // 16)), "av")
-            if hi % plan["ochunk"][r]:
-                continue
-            lo = hi - plan["ochunk"][r]
-            if r == 1:
+            when("corners", lo / 512)
+            cp(R("O", lo, hi), ind(R("YO", 0, M + TR), R("xl", lo // 16, hi // 16)), "av")
+            if hi % plan["ochunk"] == 0:
+                lo = hi - plan["ochunk"]
                 at = (lo + 2 * TR) % M
-                dma((T.yx[:, at:at + hi - lo], []), R("O", lo, hi), 2 * (hi - lo))
-            else:
-                dma(R("O2", lo, hi), R("O", lo, hi), 2 * (hi - lo))
+                dma((T.yx[:, at:at + hi - lo], []) if r else R("O2", lo, hi), R("O", lo, hi), 2 * (hi - lo))
         if r == 0:
+            when("sends")
             cp(R("U", 0, S), ind(R("WB", 0, W), R("el", 0, 42)), "av")
             compact(R("KK", 320, 362), "Bl", 0, S)
             ts(R("sl", 0, 42), R("KK", 320, 362), 7.5, A.add)
-            for p, at in enumerate((R("KK", 0, 64), R("AB", 0, 64), R("PT", 320, 384))):
+            for p in range(3):
                 lo = S + p * TR
+                when("twins", p)
                 for a in range(lo, lo + TR, plan["wchunk"]):
                     cp(R("U", a, a + plan["wchunk"]), ind(R("WB", 0, W), R("el", a // 16, (a + plan["wchunk"]) // 16)), "av")
-                compact(at, "Bl", lo, lo + TR)
-                ts(side("dl", p), at, 7.5, A.add)
-                cp(side("TW", p), at, "av")
+                compact(side("KK", p, at=128), "Bl", lo, lo + TR)
+                ts(side("dl", p), side("KK", p, at=128), 7.5, A.add)
         else:
+            when("twins")
             for lo, hi in chunks(plan["tchunk"], ()):
                 cp(R("SD", lo, hi), ind(R("SL", 0, W), R("el", (S + lo) // 16, (S + hi) // 16)), "av")
-                dma((T.yt[:, lo:hi], []), R("SD", lo, hi, row=0), 400)
+                dma((T.yt[:, lo:hi], []), R("SD", lo, hi, row=0), 400, 1)
     link(ops)
     return ops
 
@@ -424,8 +625,9 @@ def rank_program(g, core, T, topo):
     rank = T.rank_of(core)
     if rank is None:
         return
-    digits = "0123456789abcdefghijklmnopqrstuvwxyzABCDEFGHIJKLMNOPQRSTUVWXYZ"
-    code = [digits.index(ORDER[i]) * 62 + digits.index(ORDER[i + 1]) for i in range(0, len(ORDER), 2)]
-    emit(g, T, calls(core, rank, T, topo, PLAN), [(v // 5, "vapgs"[v % 5]) for v in code])
+    ops = calls(core, rank, T, topo, PLAN)
+    if not DEALT:
+        DEALT.extend(deal(ops, PLAN))
+    emit(g, T, ops, DEALT)
     for r in range(2):
         g.wait_ge(T.sem["snt%d" % r], N - 1)

@@ -8,8 +8,8 @@ MID = 7.5 * WC
 BIG = float(2 ** 25)
 FAR = 32768.0
 R16 = 1.5 * 2 ** 27
-SCALES = [1.0, -1.0, 0.0, float(WC), 1.0 / 16, 1024.0, -1024.0, 3072.0, -192.0]
-DUP = 2
+SCALES = [1.0, -1.0, float(WC), 1.0 / 16, 1024.0, -1024.0, 3072.0, -192.0]
+LEAD = (16, M)
 LISTS = ("sel", "hi", "dlo", "b16", "low")
 
 
@@ -18,31 +18,32 @@ def _sb(dt, **k):
 
 
 SCRATCH = {}
-SCRATCH.update(_sb("bfloat16", O=W, O2=M, YO=M + TR, DM=M, come0=16 + S, come1=16 + S, give0=S, give1=S, WB=W, U=W,
-                   same=192, s0=192, s2=192, cc=256, cl=240, ones=64, fl=192, dhi=192, LS=[len(LISTS), 240],
+SCRATCH.update(_sb("bfloat16", O=W, O2=M, YO=M + TR, DM=M, come0=16 + S, come1=M + S, give0=S, give1=S, WB=W, U=W,
+                   same=192, s16=96, s0=192, s2=192, cc=256, cl=240, tie=192, fl=192, dhi=192, LS=[len(LISTS), 240],
                    Ib=128 * len(SCALES), Bs=144, Bh=144, Bl=144))
-SCRATCH.update(_sb("float16", PG=192, N1=192, N2=192, TS=192))
-SCRATCH.update(_sb("float32", SD=M, SL=W, TF=[6, 2, 16], TW=192, f2=42, LOC=240, sm=192, Z=768, ZM=256, col=16, RD=256, RG=32, RB=256,
-                   If=128, EE=64, GI=64))
-SCRATCH.update(_sb("int32", TB=[2, 6, 16], SN=42, i1=42, P=8))
+SCRATCH.update(_sb("float16", PG=192, N1=192, N2=192, TS=192, MA=192, hh=192))
+SCRATCH.update(_sb("float32", SD=M, SL=W, TF=[6, 2, 16], TW=192, f2=42, LOC=240, sm=192, Z=512, ZM=256, col=16, RD=256, RG=48, RB=256,
+                   If=128, EE=128, GI=96, B0=144, f1=42))
+SCRATCH.update(_sb("int32", TB=[2, 6, 16], SN=42, i1=42, P=12))
 SCRATCH.update(_sb("uint16", dl=192, yl=192, xl=192, el=WC, sl=42, pl=64))
 PSUM = ("A0", "A1", "G0", "G1", "G2", "KK", "S0", "S1")
 for _n in PSUM:
     SCRATCH[_n] = ("psum", [128, 512], "float32")
 NDMA = 40
 SEMAPHORES = ["cv", "ca", "cp", "cg", "arr0", "arr1", "snt0", "snt1"] + ["d%d" % _k for _k in range(NDMA)]
-PLAN = {"yact": ((2, 3, 4, 5), (3, 4, 5)), "dact": ((), ()), "dchunk": 512, "xchunk": 512, "ychunk": 512, "tchunk": 512, "wchunk": 512,
-        "ochunk": 1024, "rem": (2.7, 1.0), "remrows": 3.8, "gat": 1.56, "row": 0.02, "dma": 0.8, "wake": 0.06,
-        "tries": 220000, "seed": 1, "mean": 0.05, "heat": 0.15, "share": 1.0, "fill": 2048, "lean": 0.3, "apart": True, "give": ("v", "av"),
-        "load": ((0, 2048), (2048, 3072)),
-        "due": {"give": (3.0, 19.0, 0, 0), "digits": (2.0, 22.5, 0, 0), "slots": (9.0, 26.0, 0, 0), "rows": (8.0, 25.0, 0, 0),
-                "same": (3.0, 24.0, 0, 0), "next": (3.2, 27.0, 0, 0), "prev": (12.6, 28.6, 0, 0), "edge": (3.5, 19.5, 0.5, 0.7),
-                "twin": (5.0, 21.0, 0.7, 0.7), "key": (8.0, 24.0, 1.5, 1.5), "pos": (13.5, 29.5, 0, 0), "border": (13.0, 29.0, 0, 0),
-                "flips": (12.5, 28.5, 0, 0), "lists": (16.0, 32.0, 0, 0), "corners": (17.0, 33.0, 0.2, 0.2), "sends": (16.5, 0, 0, 0),
-                "twins": (18.5, 35.0, 1.0, 0)}}
-
-
-DEALT = []
+SIX, FOUR = (512,) * 6, (1024, 1024, 512, 512)
+PLAN = {
+    "load": (2048, 1024), "loads": "sxxt", "twin": (FOUR, FOUR), "border": ("vvaaaa", "vvaaaa"), "corners": (SIX, SIX), "twins": (SIX, (512, 512, 512, 512, 384, 384, 256)),
+    "store": (1024, 1024, 1024), "again": (0, 1, 2), "low": "v", "early": 3.2, "turn": (0, 0), "ask": (("av", "av"), ("av", "av")), "give": ((352, 320), (672,)), "rules": ("twins1",),
+    "gat": 1.56, "mm": 0.004, "row": 0.023, "dma": 1.15, "rem": (3.0, 1.2), "remrows": 5.0, "wake": 0.07,
+    "due": {"give": (0.3, 19.5, 0, 0), "digits": (8, 24, 0, 0), "slots": (11.0, 26.0, 0, 0), "rows": (11.0, 27.0, 0, 0),
+            "same": (9, 26, 0, 0), "next": (12.5, 30.5, 0, 0), "prev": (13.6, 31.6, 0, 0), "edge": (2.5, 21.5, 0.6, 0.6),
+            "sums": (6.0, 25.0, 1.0, 1.0), "twin": (5.7, 22.8, 0.7, 0.7), "key": (7.5, 26.5, 1.3, 1.3), "pos": (16.0, 34.0, 0, 0),
+            "border": (14.0, 32.0, 0, 0), "flips": (13.5, 31.5, 0, 0), "lists": (18.0, 35.5, 0, 0),
+            "corners": (18.3, 35.6, 0.2, 0.2), "sends": (18.1, 0, 0, 0), "twins": (21.3, 37.0, 0.5, 0.1)},
+    "tries": 350000, "starts": 1, "cases": ((0.9, 0.9, 1.15, 1.0), (1.15, 1.05, 0.85, 1.05)), "seed": 65, "mean": 0.1, "heat": 0.35, "mark": 0.2, "reach": 30, "look": 0.1, "cold": 0, "lean": 0,
+    "stones": ("sel", "xl", "YO")}
+DEALT, WORTH = [], []
 
 
 def meet(x, y):
@@ -68,124 +69,43 @@ def link(ops):
             touch.setdefault(r[0], set()).add(n)
 
 
-def place(ops, pre, rank, plan, back, only):
-    busy = {e: [] for e in "vapgsd"}
-    left = [len(p) for p in pre]
-    after = [[] for _ in ops]
-    for n, p in enumerate(pre):
-        for m in p:
-            after[m].append(n)
-    begin, done, at = {}, {}, {}
-    ready = [n for n in range(len(ops)) if not left[n]]
-
-    def gap(e, t, c):
-        for a, b in busy[e]:
-            if t + c <= a:
-                break
-            t = max(t, b)
-        return t
-
-    while ready:
-        n = min(ready, key=lambda n: (rank[n], n))
-        ready.remove(n)
-        o = ops[n]
-        best = None
-        for e in only.get(n, o["alt"]):
-            t = max([0.0] + [done[m] + (0.0 if at[m] == e == "p" else plan["wake"]) for m in pre[n]]) + (o["lat"] if back else 0.0)
-            use = [(e, o["c"])] if o["kind"] == "c" else [(e, 0.05), ("d", o["c"])]
-            if o["kind"] == "rem" and plan["apart"]:
-                use = [(e, 0.3)]
-            while True:
-                u = max(gap(x, t, c) for x, c in use)
-                if u == t:
-                    break
-                t = u
-            t2 = t + (plan["lean"] if e == "v" and len(o["alt"]) > 1 else 0.0)
-            if best is None or t2 < best[0]:
-                best = (t2, t, e, use)
-        _, t, e, use = best
-        for x, c in use:
-            busy[x].append((t, t + c))
-            busy[x].sort()
-        begin[n], done[n], at[n] = t, t + o["c"] + (0.0 if back else o["lat"]), e
-        for m in after[n]:
-            left[m] -= 1
-            if not left[m]:
-                ready.append(m)
-    return begin, done, at
-
-
-def deal(ops, plan):
-    pre, above = [], []
-    for o in ops:
-        p = [m for m, _ in o["pre"]]
-        far = set().union(*(above[m] for m in p))
-        pre.append([m for m in p if m not in far])
-        above.append(far.union(p))
-    post = [[] for _ in ops]
-    rank = [o["due"] for o in ops]
-    for n in reversed(range(len(ops))):
-        for m in pre[n]:
-            rank[m] = min(rank[m], rank[n] - 1e-6)
-            post[m].append(n)
-    best = None
-    for _ in range(plan["passes"]):
-        begin, done, at = place(ops, pre, rank, plan, False, {})
-        worth = max(done.values()) + plan["mean"] * sum(done.values()) / len(ops)
-        if best is None or worth < best[0]:
-            best = (worth, begin, at, rank, {})
-        _, done, _ = place(ops, post, [-done[n] for n in range(len(ops))], plan, True, {})
-        rank = [-done[n] for n in range(len(ops))]
-    seed = plan["seed"]
-    now = best
-    for i in range(plan["tries"]):
-        rank, only = [now[1][n] for n in range(len(ops))], dict(now[4])
-        seed = (seed * 1103515245 + 12345) % 2 ** 31
-        n, k = seed // 64 % len(ops), seed // 2 ** 20 % 16
-        if len(ops[n]["alt"]) > 1 and k < 6:
-            only[n] = ("a", "v", "av")[k % 3]
-        else:
-            new = rank[n] + (k - 9.5) * abs(k - 9.5) * plan["jump"]
-            for m in above[n]:
-                rank[m] = min(rank[m], new - 1e-3 * (rank[n] - rank[m]))
-            rank[n] = new
-        begin, done, at = place(ops, pre, rank, plan, False, only)
-        worth = max(done.values()) + plan["mean"] * sum(done.values()) / len(ops)
-        if worth <= now[0] + plan["heat"] * (1 - i / plan["tries"]) * (seed // 2 ** 24 % 8) / 8:
-            now = (worth, begin, at, rank, only)
-            if worth < best[0]:
-                best = now
-    return [(n, best[2][n]) for n in sorted(best[1], key=lambda n: (best[1][n], n))]
-
-
-def play(ops, pre, order, at, plan):
-    free = {e: 0.0 for e in "vapgsd"}
-    last, done, by = {}, {}, {}
+def play(ops, pre, order, at, plan, old=None, first=0):
     wake = plan["wake"]
-    for n in order:
-        o, e = ops[n], at[n]
-        t, x, held = free[e], last.get(e), True
+    first -= first % 32
+    if first:
+        marks, done, by = old[2][:first // 32], list(old[3]), list(old[4])
+        free, last = dict(old[2][first // 32][0]), dict(old[2][first // 32][1])
+    else:
+        marks, done, by = [], [0.0] * len(ops), [None] * len(ops)
+        free, last = {e: 0.0 for e in "vapgsd"}, {e: None for e in "vapgsd"}
+    for i in range(first, len(order)):
+        if i % 32 == 0:
+            marks.append((dict(free), dict(last)))
+        n = order[i]
+        c, lat, hold = ops[n]
+        e = at[n]
+        t, x, held = free[e], last[e], True
         for m in pre[n]:
             u = done[m] if e == "p" == at[m] else done[m] + wake
             if u > t:
                 t, x, held = u, m, False
-        if o["kind"] == "c":
-            done[n] = free[e] = t + o["c"]
+        if hold is None:
+            done[n] = free[e] = t + c
         else:
-            free[e] = t + o["hold"]
-            if free["d"] > t + o["lat"] / 2:
-                t, x, held = free["d"] - o["lat"] / 2, last["d"], True
-            free["d"] = t + o["lat"] / 2 + o["c"] * (plan["share"] if o["kind"] == "rem" else 1)
-            done[n] = t + o["lat"] + o["c"]
+            free[e] = t + hold
+            if free["d"] > t + lat / 2:
+                t, x, held = free["d"] - lat / 2, last["d"], True
+            free["d"] = t + lat / 2 + c
+            done[n] = t + lat + c
             last["d"] = n
         last[e] = n
         by[n] = (x, held)
-    n = max(done, key=done.get)
-    worth, path = done[n] + plan["mean"] * sum(done.values()) / len(done), []
+    end = max(done)
+    n, path = done.index(end), []
     while n is not None:
         path.append((n, by[n][0] if by[n][1] else None))
         n = by[n][0]
-    return worth, path
+    return end + plan["mean"] * sum(done) / len(done) + plan["mark"] * sum(done[n] for n in plan["marks"]), path, marks, done, by
 
 
 def deal(ops, plan):
@@ -194,14 +114,60 @@ def deal(ops, plan):
         p = [m for m, _ in o["pre"]]
         far = set().union(*(above[m] for m in p))
         pre.append([m for m in p if m not in far])
-        above.append(far.union(p))
+        above.append(far.union(p, o.get("behind", ()), *(above[m] for m in o.get("behind", ()))))
     rank = [o["due"] for o in ops]
     for n in reversed(range(len(ops))):
-        for m in pre[n]:
+        for m in pre[n] + list(ops[n].get("behind", ())):
             rank[m] = min(rank[m], rank[n] - 1e-6)
     order = sorted(range(len(ops)), key=lambda n: rank[n])
-    at = {n: o["alt"][0] for n, o in enumerate(ops)}
-    now = play(ops, pre, order, at, plan)
+    at = [o["alt"][0] for o in ops]
+    both = [len(o["alt"]) > 1 for o in ops]
+    costs = [(o["c"], o["lat"], o["hold"]) for o in ops]
+    if plan["look"]:
+        order, done, since, free = [], {}, {}, {e: 0.0 for e in "vapgsd"}
+        left = [set(pre[n]).union(o.get("behind", ())) for n, o in enumerate(ops)]
+        after = [[] for _ in ops]
+        for n, p in enumerate(left):
+            for m in p:
+                after[m].append(n)
+        fresh, ready = [n for n, p in enumerate(left) if not p], []
+        while fresh or ready:
+            for n in fresh:
+                since[n] = max([0.0] + [done[m] + plan["wake"] for m in pre[n]])
+            ready = sorted(ready + fresh, key=lambda n: rank[n])
+            pick = []
+            for e in "vapgs":
+                mine = [n for n in ready if e in ops[n]["alt"]
+                        and not (e == "v" and both[n] and free["a"] <= max(free["v"], since[n]) + plan["lean"])]
+                if mine:
+                    t = max(free[e], min(since[n] for n in mine))
+                    n = next(n for n in mine if since[n] <= t + plan["look"] * (8 if e == "g" else 1))
+                    pick.append((t, rank[n], n, e))
+            t, _, n, e = min(pick)
+            t = max(t, since[n])
+            c, lat, hold = costs[n]
+            if hold is None:
+                done[n] = free[e] = t + c
+            else:
+                free[e] = t + hold
+                free["d"] = max(free["d"], t + lat / 2) + c
+                done[n] = free["d"] + lat / 2
+            at[n] = e
+            order.append(n)
+            ready.remove(n)
+            for m in after[n]:
+                left[m].discard(n)
+            fresh = [m for m in after[n] if not left[m]]
+    marks = [n for n, o in enumerate(ops) if o["kind"] == "rem" or any(w[0] in plan["stones"] for w in o["w"])]
+    plan = dict(plan, marks=marks, mark=plan["mark"] / len(marks))
+    cases = [[(c * (rows if o["kind"] == "rem" else gat if o.get("gather") else mm if o["alt"] == "p" else 1), lat * late, hold)
+              for o, (c, lat, hold) in zip(ops, costs)] for rows, late, gat, mm in plan["cases"]]
+
+    def plays(order, at, old, first):
+        each = [play(c, pre, order, at, plan, old and old[1][k], first) for k, c in enumerate(cases)]
+        return sum(x[0] for x in each) / len(each), each
+
+    now = plays(order, at, None, 0)
     best = (now[0], order, at)
     seed = [plan["seed"]]
 
@@ -209,37 +175,49 @@ def deal(ops, plan):
         seed[0] = (seed[0] * 1103515245 + 12345) % 2 ** 31
         return seed[0] // 256 % k
 
-    for i in range(plan["tries"]):
-        n, m = now[1][draw(len(now[1]))]
+    begin = (now, order, at)
+    for i in range(plan["tries"] * plan["starts"]):
+        i %= plan["tries"]
+        if i == 0:
+            now, order, at = begin
+        _, path, _, _, by = now[1][draw(len(cases))]
+        if draw(2):
+            n, path = marks[draw(len(marks))], []
+            while n is not None and len(path) < plan["reach"]:
+                path.append((n, by[n][0] if by[n][1] else None))
+                n = by[n][0]
+        n, m = path[draw(len(path))]
         k = draw(16)
         o2, a2 = order, at
         if k < 3:
-            n = draw(len(ops))
-            same = [x for x in order[:order.index(n)] if at[x] == at[n]]
-            m = same[-1] if same else None
-        if len(ops[n]["alt"]) > 1 and k % 4 == 0:
-            a2 = dict(at)
+            b = draw(len(ops))
+            n = order[b]
+            m = next((x for x in order[b - 1::-1] if at[x] == at[n]), None) if b else None
+        if both[n] and k % 4 == 0:
+            a = order.index(n)
+            a2 = list(at)
             a2[n] = "a" if at[n] == "v" else "v"
             if k >= 8:
-                b = order.index(n)
-                near = [x for x in order[max(0, b - 25):b + 25] if len(ops[x]["alt"]) > 1 and at[x] == a2[n]]
+                near = [x for x in order[max(0, a - 25):a + 25] if both[x] and at[x] == a2[n]]
                 if near:
                     a2[near[draw(len(near))]] = at[n]
+                    a = max(0, a - 25)
         elif m is None or m in above[n]:
             continue
         else:
             a, b = order.index(m), order.index(n)
             if k % 2:
-                first = [x == n or x in above[n] for x in order[a:b + 1]]
+                front = [x == n or x in above[n] for x in order[a:b + 1]]
             else:
-                first = [not (x == m or m in above[x]) for x in order[a:b + 1]]
-            o2 = (order[:a] + [x for x, f in zip(order[a:b + 1], first) if f] + [x for x, f in zip(order[a:b + 1], first) if not f]
+                front = [not (x == m or m in above[x]) for x in order[a:b + 1]]
+            o2 = (order[:a] + [x for x, f in zip(order[a:b + 1], front) if f] + [x for x, f in zip(order[a:b + 1], front) if not f]
                   + order[b + 1:])
-        new = play(ops, pre, o2, a2, plan)
-        if new[0] <= now[0] + plan["heat"] * (1 - i / plan["tries"]) * draw(8) / 8:
+        new = plays(o2, a2, now, a)
+        if new[0] <= now[0] + (k >= plan["cold"]) * plan["heat"] * (1 - i / plan["tries"]) * draw(8) / 8:
             now, order, at = new, o2, a2
             if now[0] < best[0]:
                 best = (now[0], order, at)
+    WORTH.append(best[0])
     return [(n, best[2][n]) for n in best[1]]
 
 
@@ -296,9 +274,9 @@ def calls(core, rank, T, topo, plan):
         now[0] = t
 
     def R(name, lo, hi, step=1, row=None):
-        part = slice(0, 128) if row is None else slice(row, 128, 16)
         if name in LISTS:
             return (T.LS[:, LISTS.index(name), lo:hi], [(name, lo, hi, None)], hi - lo, 2)
+        part = slice(0, 128) if row is None else slice(row, 128, 16)
         ap = T[name][part, lo:hi] if step == 1 else T[name][part, lo:hi:step]
         return (ap, [(name, lo, hi, row)], len(range(lo, hi, step)), 4 if SCRATCH[name][2].endswith("32") else 2)
 
@@ -307,7 +285,7 @@ def calls(core, rank, T, topo, plan):
 
     def add(e, kind, fn, w, r, c, lat=0.0, ext=()):
         ops.append({"alt": e, "kind": kind, "fn": fn, "w": list(w), "r": list(r), "ext": list(ext), "c": c, "lat": lat,
-                    "due": now[0] + 1e-4 * len(ops), "hold": 0.05 if kind == "dma" else lat - 0.7})
+                    "due": now[0] + 1e-4 * len(ops), "hold": {"c": None, "dma": 0.05, "rem": lat - 0.7}[kind]})
 
     def cost(out, a, cycles=1.0):
         return 0.055 + 0.83e-3 * (plan["gat"] * a[2] if a[3] == 0 else max(64, out[2] * cycles))
@@ -315,6 +293,7 @@ def calls(core, rank, T, topo, plan):
     def tt(out, a, b, op, ext=()):
         both = a[1][0][0] not in PSUM and b[1][0][0] not in PSUM
         add("v", "c", lambda q, e: q.tensor_tensor(out[0], a[0], b[0], op), out[1], a[1] + b[1], cost(out, a, 2 if both else 1), 0.0, ext)
+        ops[-1]["gather"] = a[3] == 0
 
     def ts(out, a, s1, op0, s2=None, op1=None):
         r = list(a[1]); v = []
@@ -332,17 +311,22 @@ def calls(core, rank, T, topo, plan):
     def cp(out, a, e="v", ext=()):
         add(e, "c", lambda q, e: q.tensor_copy(out[0], a[0]) if e == "v" else q.activation(out[0], a[0], F.Copy), out[1], a[1],
             cost(out, a), 0.0, ext)
+        ops[-1]["gather"] = a[3] == 0
 
-    def act(out, a, func, scale=1.0, bias=None):
-        if bias is None:
-            add("a", "c", lambda q, e: q.activation(out[0], a[0], func, scale=scale), out[1], a[1], cost(out, a))
-        else:
-            add("a", "c", lambda q, e: q.activation(out[0], a[0], func, bias=bias, scale=scale), out[1], a[1], cost(out, a))
+    def square(out, a):
+        add("a", "c", lambda q, e: q.activation(out[0], a[0], F.Square), out[1], a[1], cost(out, a))
+
+    def relu(out, a):
+        add("av", "c", lambda q, e: q.tensor_scalar(out[0], a[0], 0.0, None, A.max) if e == "v" else q.activation(out[0], a[0], F.Relu),
+            out[1], a[1], cost(out, a))
 
     def affine(out, a, mul, plus):
-        b, r = (plus[0], plus[1]) if isinstance(plus, tuple) else (plus, [])
-        add("av", "c", lambda q, e: q.tensor_scalar(out[0], a[0], mul, b, A.mult, A.add) if e == "v"
-            else q.activation(out[0], a[0], F.Identity, bias=b, scale=mul), out[1], a[1] + r, cost(out, a))
+        (m, rm), (b, rb) = ((s[0], s[1]) if isinstance(s, tuple) else (s, []) for s in (mul, plus))
+        add("av", "c", lambda q, e: q.tensor_scalar(out[0], a[0], m, b, A.mult, A.add) if e == "v"
+            else q.activation(out[0], a[0], F.Identity, bias=b, scale=m), out[1], a[1] + rm + rb, cost(out, a))
+
+    def act(out, a, func, scale, bias):
+        add("a", "c", lambda q, e: q.activation(out[0], a[0], func, bias=bias, scale=scale), out[1], a[1], cost(out, a))
 
     def group(out, terms, start=True, stop=True):
         def fn(q, e):
@@ -350,10 +334,7 @@ def calls(core, rank, T, topo, plan):
                 ins = q.matmul((t[2] if len(t) > 2 else out)[0], t[0][0], t[1][0], start and k == 0, stop and k == len(terms) - 1)
             return ins
         add("p", "c", fn, out[1], sum((t[0][1] + t[1][1] for t in terms), []),
-            sum(0.417e-3 * max(64, t[1][2]) * (4 if t[0][3] == 4 else 1) for t in terms))
-
-    def ms(out, c):
-        add("v", "c", lambda q, e: q.memset(out[0], c), out[1], [], cost(out, out, out[3] / 4))
+            sum(plan["mm"] + 0.417e-3 * max(64, t[1][2]) * (4 if t[0][3] == 4 else 1) for t in terms))
 
     def iota(out, pat, base=0, cm=0, small=True):
         c = 0.13 + 1.66e-3 * out[2]
@@ -368,71 +349,78 @@ def calls(core, rank, T, topo, plan):
     def side(name, p, n=64, at=0):
         return R(name, at + (p % 3) * n, at + (p % 3 + 1) * n)
 
-    def chunks(step, skip):
-        out = []
-        for lo in range(0, M, min(step, 512)):
-            if lo // 512 not in skip:
-                if out and out[-1][1] == lo and lo % step:
-                    out[-1][1] += 512
-                else:
-                    out.append([lo, lo + min(step, 512)])
-        return out
+    def cut(sizes):
+        return [(sum(sizes[:k]), sum(sizes[:k + 1])) for k in range(len(sizes))]
 
     col = lambda k: R("col", k, k + 1)
     Ib = lambda k: R("Ib", 128 * k, 128 * k + 128)
-    I1, IN, ZERO, IW, I16, K1, KN, K3, N192 = (Ib(k) for k in range(len(SCALES)))
+    I1, IN, IW, I16, K1, KN, K3, N192 = (Ib(k) for k in range(len(SCALES)))
     IF = R("If", 0, 128)
 
-    for gl in range(2):
-        dma((T.TB[:, gl], [("TB", gl, gl + 1, None)]), (T.twn[gl:8:2, :], []), 384)
-    dma(R("SN", 0, 42), (T.snd[:, :], []), 168)
-    for lo, hi in plan["load"]:
-        dma(R("O", (lo + TR) % M, (lo + TR) % M + hi - lo), (T.x[:, lo:hi], []), 2 * (hi - lo))
+    pieces = cut(plan["load"])
+    for what in plan["loads"]:
+        if what == "t":
+            for gl in range(2):
+                dma((T.TB[:, gl], [("TB", gl, gl + 1, None)]), (T.twn[gl:8:2, :], []), 384)
+                ops[-1]["behind"] = range(len(ops) - 1)
+        elif what == "s":
+            dma(R("SN", 0, 42), (T.snd[:, :], []), 168)
+        else:
+            lo, hi = pieces.pop(0)
+            dma(R("O", (lo + TR) % M, (lo + TR) % M + hi - lo), (T.x[:, lo:hi], []), 2 * (hi - lo))
+        ops[-1]["behind"] = range(len(ops) - 1)
     for p in range(3):
-        dma(side("O2", p, TR), (T.x[:, (p + 2) % 3 * TR:((p + 2) % 3 + 1) * TR], []), 2 * TR)
+        if p in plan["again"]:
+            dma(side("WB", p, TR), (T.x[:, (p + 2) % 3 * TR:((p + 2) % 3 + 1) * TR], []), 2 * TR)
+            ops[-1]["behind"] = range(len(ops) - 1)
+        else:
+            due(2.5 + (p - 1) % 3 * 0.5)
+            add("v", "c", lambda q, e, p=p: q.tensor_copy(side("WB", p, TR)[0], side("O", p, TR)[0]), side("WB", p, TR)[1],
+                side("O", p, TR)[1], 0.48)
+            due(0.0)
 
     iota(R("P", 0, 1), [[0, 1]], 0, 1, small=False)
+    iota(R("P", 1, 2), [[0, 1]], 0, 8, small=False)
     iota(R("RD", 0, 256), [[1, 256]])
-    iota(R("RG", 0, 8 * DUP), [[1, 8], [0, DUP]])
-    iota(R("RB", 0, 64 * DUP), [[0, 4 * DUP], [1, DUP], [0, 16 // DUP]])
+    iota(R("RG", 0, 16), [[1, 8], [0, 2]])
+    iota(R("RB", 0, 128), [[0, 8], [8, 2], [0, 8]])
     iota(R("cc", 0, 256), [[16, 256]])
-    iota(R("ones", 0, 64), [[0, 64]], 1)
-    iota(R("WB", 0, plan["fill"]), [[0, plan["fill"]]])
-    due(6.0)
-    iota(R("WB", plan["fill"], W), [[0, W - plan["fill"]]])
-    for r in range(2):
-        iota(R("come%d" % r, 0, 16), [[0, 16]], -256)
-    iota(R("SL", M, W), [[0, S]])
+    iota(R("tie", 0, 192), [[-1, 3], [0, 64]], -1)
+    iota(R("come0", 0, 16), [[0, 16]], -256)
+    iota(R("O", M, W), [[0, S]], int(FAR))
+    add("v", "c", lambda q, e: q.memset(T.LS[:, :, 192:240], 0.0), [(nm, 192, 240, None) for nm in LISTS], [], 0.155)
+    due(3.15)
+    cp(R("WB", M, W), R("O", M, W), "av")
     due(1.0)
-    ms(R("O", M, W), FAR)
-    ts(R("P", 1, 2), R("P", 0, 1), DUP - 1, A.bitwise_and)
-    ts(R("P", 2, 3), R("P", 0, 1), DUP // 2, A.arith_shift_right)
-    ts(R("P", 3, 4), R("P", 0, 1), 4, A.arith_shift_right)
-    ts(R("P", 4, 5), R("P", 0, 1), 15, A.bitwise_and)
-    cp(R("col", 0, 5), R("P", 0, 5))
+    ts(R("P", 2, 4), R("P", 0, 2), 4, A.arith_shift_right)
+    ts(R("P", 4, 6), R("P", 0, 2), 15, A.bitwise_and)
+    cp(R("col", 0, 6), R("P", 0, 6))
     ts(IF, R("RD", 0, 128), col(0), A.is_equal)
     for n, s in enumerate(SCALES):
         affine(Ib(n), IF, s, 0.0)
-    ts(R("GI", 0, 8 * DUP), R("RG", 0, 8 * DUP), col(3), A.is_equal)
-    affine(R("GI", 32, 32 + 8 * DUP), R("GI", 0, 8 * DUP), -1.0, 0.0)
+    ts(R("GI", 0, 16), R("RG", 0, 16), col(2), A.is_equal)
+    affine(R("GI", 16, 32), R("GI", 0, 16), -1.0, 0.0)
     affine(col(9), col(4), 1.0, -7.5)
     affine(R("cl", 0, 240), R("RD", 0, 240), 0.0, col(9))
+    affine(col(11), col(4), 1.0, -M / 2)
+    ts(R("hh", 0, 192), R("cc", 0, 192), col(11), A.add)
     due(3.0)
-    ts(R("ZM", 0, 64 * DUP), R("RB", 0, 64 * DUP), col(1), A.is_equal)
-    ts(R("EE", 0, 128 // DUP), R("RD", 0, 128 // DUP), col(2), A.is_equal, 4.0, A.mult)
-    add("v", "c", lambda q, e: q.memset(T.LS[:, :, 192:240], 0.0), [(nm, 192, 240, None) for nm in LISTS], [], 0.155)
-    affine(col(5), col(3), 16.0, 15.0)
-    ts(col(6), col(4), 0.0, A.is_equal)
+    ts(R("ZM", 0, 128), R("RB", 0, 128), col(5), A.is_equal)
+    ts(R("EE", 0, 64), R("RD", 0, 64), col(3), A.is_equal, 4.0, A.mult)
+    due(11.0)
+    affine(col(12), col(2), 16.0, 15.0)
+    ts(R("B0", 0, 144), R("RD", 0, 144), col(12), A.is_equal)
+    act(col(6), col(4), F.Relu, -1.0, 1.0)
     ts(col(7), col(4), 1.0, A.is_equal, float(WC), A.mult)
     ts(col(8), col(4), 2.0, A.is_equal, 1.0 / 16, A.mult)
     affine(col(7), col(8), 1.0, col(7))
-    ts(col(10), col(4), 2.5, A.is_gt)
+    act(col(10), col(4), F.Abs, 1.0, -4.5)
+    act(col(10), col(10), F.Relu, -1.0, 2.0)
+    act(col(10), col(10), F.Sign, 1.0, 0.0)
     for nm, k in (("Bs", 6), ("Bh", 7), ("Bl", 10)):
-        ts(R(nm, 0, 144), R("RD", 0, 144), col(5), A.is_equal, col(k), A.mult)
-    due(7.0)
+        affine(R(nm, 0, 144), R("B0", 0, 144), col(k), 0.0)
+    due(14.0)
     affine(R("LOC", 192, 240), R("RD", 192, 240), 16.0, col(4))
-    dma(R("WB", 0, W, row=3), R("cc", 0, WC), 468)
-    dma(R("WB", 0, W, row=4), R("cl", 0, WC), 468)
 
     due(0.5)
     for gl in range(2):
@@ -442,102 +430,118 @@ def calls(core, rank, T, topo, plan):
         add("v", "c", lambda q, e, b=b: q.transpose(T.TW[:, b:192:6], T.TF[:, b]), [("TW", 0, 192, b)], [("TF", 0, 2, None)], 0.11)
     cp(R("sl", 0, 42), R("SN", 0, 42))
     ts(R("dl", 0, 192), R("TW", 0, 192), 7.5, A.add)
-    due(8.0)
-    ts(R("i1", 0, 42), R("SN", 0, 42), 15, A.bitwise_and)
-    ts(R("f2", 0, 42), R("i1", 0, 42), 16.0 * WC - 1, A.mult)
-    tt(R("f2", 0, 42), R("f2", 0, 42), R("SN", 0, 42), A.add)
-    ts(R("el", 0, 42), R("f2", 0, 42), 1.0 / 16, A.mult)
+    due(12.0)
+    ts(R("f1", 0, 42), R("SN", 0, 42), -7.5, A.add)
+    act(R("f2", 0, 42), R("f1", 0, 42), F.Identity, 1.0, R16)
+    act(R("s16", 0, 42), R("f2", 0, 42), F.Identity, 1.0, -R16)
+    group(R("S1", 384, 426), [(IF, R("f1", 0, 42)), (IN, R("s16", 0, 42))])
+    cp(R("s16", 48, 90), R("S1", 384, 426), "a")
+    group(R("S1", 448, 490), [(I16, R("s16", 0, 42)), (IW, R("s16", 48, 90))])
+    ts(R("el", 0, 42), R("S1", 448, 490), MID, A.add)
 
     PHI, TN = R("KK", 0, 64), R("G2", 320, 384)
+    turned = lambda I, nm, to, at: [(I, R(nm, 0, 128), R(to, at + 64, at + 192)), (I, R(nm, 128, 192), R(to, at, at + 64))]
     key = lambda p: R("G%d" % p, 256, 320)
-    own = lambda q: [(I1, side("cc", q)), (I1, R("cl", 0, 64))]
-    far = lambda q: [(I1, side("dlo", q)), (I1, side("dhi", q))]
-    times = lambda k, a: [(K1 if k > 0 else KN, a)] * abs(k)
+    OWN = (I1, R("hh", 0, 192))
+    times = lambda k, a, to: [(K1 if k > 0 else KN, a, to)] * abs(k)
     stage = [0]
 
     def staging():
         stage[0] += 1
-        return "A%d" % (1 - stage[0] % 2)
+        return R("A%d" % (1 - stage[0] % 2), 0, 512)
 
     def reduce(p, first):
-        nm, gi, n, step = ("SL", 0) if first else ("SD", 32), None, 2 * TR // DUP, 16 // DUP
-        for h in range(DUP // 2):
-            terms = [(R(nm[0], p * TR + h * n + j, p * TR + h * n + n, step), R("GI", nm[1], nm[1] + 8 * DUP),
-                      R("G%d" % p, 128 * h + j, 128 * h + 128, step)) for j in range(step)]
-            start = first and h == 0
-            group(R("G%d" % p, 0, 64 * DUP), ([(ZERO, R("cc", 0, 64 * DUP))] if start else []) + terms, start,
-                  not first and h == DUP // 2 - 1)
+        nm, gi = ("SL", 0) if first else ("SD", 16)
+        terms = [(R(nm, p * TR + j, (p + 1) * TR, 8), R("GI", gi, gi + 16), R("G%d" % p, j, 128, 8)) for j in range(8)]
+        group(R("G%d" % p, 0, 128), terms, first, not first)
 
-    def compact(out, B, lo, hi):
-        group(out, [(R(B, 15 - i, 143 - i), R("U", lo + i, hi, 16)) for i in range(16)])
+    def compact(out, B, lo, hi, more=()):
+        group(out, list(more) + [(R(B, 15 - i, 143 - i), R("U", lo + i, hi, 16)) for i in range(16)])
 
-    for r in range(2):
-        TW = R("TW", 0, 192) if r == 0 else R("KK", 128, 320)
-        come = R("come%d" % r, 0, 16 + S)
-        come = (come[0], come[1] + [("arr%d" % r, 0, 1, None)], come[2], come[3])
-        arr = [("arr%d" % r, N - 1)]
-        when = lambda step, k=0, r=r: due(plan["due"][step][r] + k * plan["due"][step][2 + r])
-        when("give")
-        cp(R("give%d" % r, 0, S), ind(R("O", 0, M), R("sl", 0, 42)), plan["give"][r])
+    def give(r):
+        due(plan["due"]["give"][r])
+        for lo, hi in cut(plan["give"][r]):
+            cp(R("give%d" % r, lo, hi), ind(R("O", 0, M), R("sl", lo // 16, hi // 16)), "va")
         trs = []
         for d in range(1, N):
             dst = T.cores[(rank + d) % N]
             rid, pid = topo.addr(dst, core)
             trs.append(RemoteDMATransfer(dst_ids=[DstId(rid=rid, pnc=pid)], dma_engine_mask=1 << topo.engines(core, dst)[d - 1],
                                          remote_sem=T.sem["arr%d" % r], src=T["give%d" % r][:, (d - 1) * C:d * C],
-                                         dst=T["come%d" % r][:, 16 + (d - 1) * C:16 + d * C]))
+                                         dst=T["come%d" % r][:, LEAD[r] + (d - 1) * C:LEAD[r] + d * C]))
         add("g", "rem", lambda q, e, trs=trs, r=r: q.remote_dma_fused(trs, local_sem=T.sem["snt%d" % r]), [("arr%d" % r, 0, 1, None)],
             [("give%d" % r, 0, S, None)], plan["remrows"], plan["rem"][r])
+
+    def behind(rule, first, names):
+        if rule in plan["rules"]:
+            for o in ops[first:]:
+                o["behind"] = [n for n in range(first) if any(w[0] in names for w in ops[n]["w"])]
+
+    give(0)
+    due(6.0)
+    first = len(ops)
+    iota(R("come1", 0, M), [[0, M]], -256)
+    iota(R("SL", M, W), [[0, S]])
+    for n in range(first, len(ops)):
+        ops[n]["behind"] = [n - 1]
+    for r in range(2):
+        TW = R("TW", 0, 192) if r == 0 else R("KK", 128, 320)
+        come, yl = R("come%d" % r, 0, LEAD[r] + S), ("yl", "dl")[r]
+        come = (come[0], come[1] + [("arr%d" % r, 0, 1, None)], come[2], come[3])
+        arr = [("arr%d" % r, N - 1)]
+        when = lambda step, k=0, r=r: due(plan["due"][step][r] + k * plan["due"][step][2 + r])
         when("digits")
         ts(R("b16", 0, 192), TW, R16, A.add, R16, A.subtract)
-        tt(R("low", 0, 192), TW, R("b16", 0, 192), A.subtract)
+        if r == 0 and plan["low"] == "p":
+            group(R("KK", 128, 320), [(IF, TW), (IN, R("b16", 0, 192))])
+            cp(R("low", 0, 192), R("KK", 128, 320), "av")
+        else:
+            tt(R("low", 0, 192), TW, R("b16", 0, 192), A.subtract)
         ts(R("s0", 0, 192), R("b16", 0, 192), TR - 8.0, A.is_lt)
         ts(R("s2", 0, 192), R("b16", 0, 192), 2 * TR - 8.0, A.is_gt)
         when("slots")
-        ts(R("yl", 0, 192), TW, 23.5 - M, A.add, 15.0, A.max)
-        when("rows")
-        for row, nm in ((1, "low"), (2, "b16")):
-            dma(R("WB", 0, W, row=row), R(nm, 0, WC), 468)
+        if r == 0:
+            ts(R("yl", 0, 192), TW, 23.5 - M, A.add, 15.0, A.max)
         when("same")
-        for p in range(3):
-            group(side("KK", p, at=320), own(1) + [(IN, side("b16", p)), (IN, side("low", p)), (KN, side("s0", p)), (K1, side("s2", p))])
-        ts(R("same", 0, 192), R("KK", 320, 512), 0.0, A.is_equal, -BIG, A.mult)
+        Z = R("KK", 320, 512)
+        group(Z, [(IN, R("b16", 0, 192)), (IN, R("low", 0, 192)), (KN, R("s0", 0, 192)), (K1, R("s2", 0, 192))]
+              + [(I1, side("hh", 1), side("KK", p, at=320)) for p in range(3)])
+        ts(R("same", 0, 192), Z, 7.5 - M / 2, A.is_equal, -BIG, A.mult)
         when("next")
-        for q in range(3):
-            group(side("S0", q, at=256), [(IW, side("low", q - 1)), (I16, side("b16", q - 1)), (N192, side("s2", q - 1))])
+        group(R("S0", 256, 448), turned(IW, "low", "S0", 256) + turned(I16, "b16", "S0", 256) + turned(N192, "s2", "S0", 256))
         when("prev")
-        for q in range(3):
-            group(side("S1", q), [(I1, side("low", q - 1)), (IN, R("cl", 0, 64))])
-            group(side("S1", q, at=192), [(I1, side("b16", q - 1)), (K3, side("s0", q - 1)), (IN, R("cc", 64 * q + 64, 64 * q + 128))])
+        at = 0 if r else 192
+        low = [(IN, R("cl", 0, 192), R("S1", 0, 192))] + turned(I1, "low", "S1", 0)
+        high = turned(I1, "b16", "S1", at) + turned(K3, "s0", "S1", at)
+        high += [(IN, R("cc", 128, 192), side("S1", q)) for q in range(3)] if r else [(IN, R("cc", 64, 256), R("S1", 192, 384))]
+        group(R("S1", 0, 384), low + high)
         for p in range(3):
             for h in range(2):
                 when("edge", 2 * p + h)
-                s = R(staging(), 0, 512)
+                s = staging()
                 group(s, [(I1, R("O", (p + 1) % 3 * TR + 512 * h, (p + 1) % 3 * TR + 512 * h + 512)),
                           (IN, R("O", (p + 2) % 3 * TR + 512 * h, (p + 2) % 3 * TR + 512 * h + 512))])
-                act(R("SL", p * TR + 512 * h, p * TR + 512 * h + 512), s, F.Square)
+                square(R("SL", p * TR + 512 * h, p * TR + 512 * h + 512), s)
+                if r == 0 and 2 * p + h > 0:
+                    behind("give", len(ops) - 1, ("give0",))
+            when("sums", p)
             reduce(p, True)
-        for lo, hi in chunks(plan["dchunk"], plan["dact"][r]):
+        for lo, hi in cut(plan["twin"][r]):
             when("twin", lo / 512)
-            tt(R("SD", lo, hi), ind(R("O", 0, W), R("dl", lo // 16, hi // 16)), R("O2", lo, hi), A.subtract)
-            act(R("SD", lo, hi), R("SD", lo, hi), F.Square)
-        for n in plan["dact"][r]:
-            lo, hi = 512 * n, 512 * n + 512
-            cp(R("DM", lo, hi), ind(R("O", 0, W), R("dl", lo // 16, hi // 16)), "a")
-            s = R(staging(), 0, 512)
-            group(s, [(I1, R("DM", lo, hi)), (IN, R("O", lo, hi))])
-            act(R("SD", lo, hi), s, F.Square)
+            tt(R("SD", lo, hi), ind(R("O", 0, W), R("dl", lo // 16, hi // 16)), R("O2" if r else "WB", lo, hi), A.subtract)
+            square(R("SD", lo, hi), R("SD", lo, hi))
+            if r == 0 and "tail" in plan["rules"]:
+                ops[-1]["also"] = [n for n, o in enumerate(ops) if ("WB", M, W, None) in o["w"]]
+        when("rows")
+        for row, nm in ((1, "low"), (2, "b16")):
+            dma(R("WB", 0, W, row=row), R(nm, 0, WC), 468)
         for p in range(3):
             when("key", p)
             reduce(p, False)
-            tt(side("Z", p, 64 * DUP), R("G%d" % p, 0, 64 * DUP), R("ZM", 0, 64 * DUP), A.mult)
-            n = 128 // DUP
-            group(key(p), [(I1, side("same", p))] + [(IN, R("ones", 0, 64))] * (p + 1)
-                  + [(R("Z", 64 * DUP * p + 128 * h, 64 * DUP * p + 128 * h + 128), R("EE", 0, n), R("G%d" % p, 256 + h * n, 256 + h * n + n))
-                     for h in range(DUP // 2)])
+            tt(side("Z", p, 128), R("G%d" % p, 0, 128), R("ZM", 0, 128), A.mult)
+            group(key(p), [(I1, side("same", p)), (I1, side("tie", p))] + [(side("Z", p, 128), R("EE", 0, 64))])
             if p == 0:
-                add("av", "c", lambda q, e: q.tensor_scalar(side("sm", 0)[0], key(0)[0], 0.0, None, A.max) if e == "v"
-                    else q.activation(side("sm", 0)[0], key(0)[0], F.Relu), side("sm", 0)[1], key(0)[1], 0.11)
+                relu(side("sm", 0), key(0))
             else:
                 tt(side("sm", p), key(p), side("sm", p - 1), A.max)
         for p in range(3):
@@ -547,57 +551,68 @@ def calls(core, rank, T, topo, plan):
         group(R("KK", 384, 448), [(I1, side("PG", p)) for p in range(3)])
         ts(R("pl", 0, 64), R("KK", 384, 448), MID + 64, A.add)
         for h in range(2):
-            cp(R("U", 512 * h, 512 * h + 512), ind(R("WB", 0, W), R("pl", 32 * h, 32 * h + 32)), "av")
+            cp(R("U", 512 * h, 512 * h + 512), ind(R("WB", 0, W), R("pl", 32 * h, 32 * h + 32)), plan["ask"][r][h])
+        if r == 0:
+            dma(R("WB", 0, W, row=3), R("cc", 0, WC), 468)
+            dma(R("WB", 0, W, row=4), R("cl", 0, WC), 468)
         compact(PHI, "Bs", 0, TR)
         compact(TN, "Bh", 0, TR)
         when("pos")
-        for k, p in enumerate((0, 1, 2, 0)):
-            group(R("S0", 64 * k, 64 * k + 64), [(IW, side("low", p)), (I16, side("b16", p))])
+        group(R("S0", 0, 256), [(IW, R("low", 0, 192), R("S0", 0, 192)), (I16, R("b16", 0, 192), R("S0", 0, 192)),
+                                (IW, R("low", 0, 64), R("S0", 192, 256)), (I16, R("b16", 0, 64), R("S0", 192, 256))])
         when("border")
-        for lo, hi in chunks(plan["ychunk"], plan["yact"][r]):
-            tt(R("YO", lo, hi), ind(come, R("yl", lo // 16, hi // 16)), R("O", lo, hi), A.max, arr)
-        for n in plan["yact"][r]:
+        for n, e in enumerate(plan["border"][r]):
             lo, hi = 512 * n, 512 * n + 512
-            cp(R("DM", lo, hi), ind(come, R("yl", lo // 16, hi // 16)), "a", arr)
-            s = R(staging(), 0, 512)
-            group(s, [(I1, R("DM", lo, hi))])
-            tt(R("YO", lo, hi), s, R("O", lo, hi), A.max)
+            if e == "v":
+                tt(R("YO", lo, hi), ind(come, R(yl, lo // 16, hi // 16)), R("O", lo, hi), A.max, arr)
+            else:
+                cp(R("DM", lo, hi), ind(come, R(yl, lo // 16, hi // 16)), "a", arr)
+                s = staging()
+                group(s, [(I1, R("O", lo, hi))])
+                tt(R("YO", lo, hi), s, R("DM", lo, hi), A.max)
         dma(R("YO", M, M + TR), R("YO", 0, TR), 2 * TR)
         fl = lambda q: side("fl", q)
         when("flips")
+        group(R("G0", 0, 192), [OWN], True, False)
+        if r:
+            group(R("G1", 0, 192), [OWN], True, False)
         for q in range(3):
             tt(fl(q), PHI, side("sel", q), A.mult)
-        tt(R("dlo", 0, 192), R("S1", 0, 192), R("fl", 0, 192), A.mult)
-        tt(R("dhi", 0, 192), R("S1", 192, 384), R("fl", 0, 192), A.mult)
-        for q in range(3):
-            back = times(((q - 1) % 3 - q), fl(q - 1))
-            group(side("G1", q), [(I1, side("dhi", q))] + back if r == 0 else own(q) + far(q) + back)
+        more = lambda q: 1 - q % 3 if r else 0
+        group(R("G0", 0, 192), sum((times((q + 1) % 3 - q + more(q + 1), fl(q + 1), side("G0", q)) + times(1 + more(q), fl(q), side("G0", q))
+                                    + times((q + 1) % 3 - q, fl(q - 1), side("G0", q)) for q in range(3)), []), False, False)
+        group(R("G1", 0, 192), sum((times((q - 1) % 3 - q, fl(q - 1), side("G1", q)) + times(more(q), fl(q), side("G1", q))
+                                    for q in range(3)), []), r == 0, False)
+        far = (("dhi", 192), ("dlo", 0)) if r == 0 else (("MA", 0),)
+        for nm, at in far:
+            tt(R(nm, 0, 192), R("S1", at, at + 192), R("fl", 0, 192), A.mult)
+        group(R("G1", 0, 192), [(I1, R(far[0][0], 0, 192))], False, True)
         if r == 0:
             cp(R("hi", 0, 192), R("G1", 0, 192), "av")
             dma(R("WB", 0, W, row=5), R("dlo", 0, WC), 468)
             dma(R("WB", 0, W, row=6), R("hi", 0, WC), 468)
         else:
-            affine(R("LOC", 0, 192), R("G1", 0, 192), 1.0, 7.5)
+            affine(R("LOC", 0, 192), R("G1", 0, 192), 1.0, M / 2)
             dma(R("SL", 0, W, row=0), R("LOC", 0, WC), 936)
-        for q in range(3):
-            group(side("G0", q), own(q) + far(q + 1) + times((q + 1) % 3 - q, fl(q + 1)) + far(q) + times(1, fl(q))
-                  + times((q + 1) % 3 - q, fl(q - 1)))
-        for lo, hi in ((0, 64), (64, 192)):
-            ts(R("xl", lo, hi), R("G0", lo, hi), 7.5, A.add)
+        group(R("G0", 0, 192), sum(([(I1, R(nm, 0, 192)), (I1, R(nm, 64, 192), R("G0", 0, 128)), (I1, R(nm, 0, 64), R("G0", 128, 192))]
+                                    for nm, _ in far), []), False, True)
+        ts(R("xl", 0, 192), R("G0", 0, 192), M / 2, A.add)
         when("lists")
+        group(R("G2", 0, 192), [(IW, R("low", 0, 192)), (I16, R("b16", 0, 192))], True, False)
+        first = len(ops)
         tt(R("N1", 0, 192), R("S0", 64, 256), R("fl", 0, 192), A.mult)
         tt(R("N2", 0, 192), R("S0", 0, 192), R("fl", 0, 192), A.mult)
         for q in range(3):
-            tt(side("TS", q), TN, fl(q), A.mult)
-        for q in range(3):
-            group(side("G2", q), [(IW, side("low", q)), (I16, side("b16", q)), (I1, side("N1", q)), (IN, side("N2", q)),
-                                  (IN, side("N1", q - 1)), (I1, side("TS", q - 1))])
+            tt(side("TS", q + 1), TN, fl(q), A.mult)
+        behind("lists%d" % r, first, ("YO", "xl"))
+        group(R("G2", 0, 192), [(I1, R("N1", 0, 192)), (IN, R("N2", 0, 192)), (I1, R("TS", 0, 192))] + turned(IN, "N1", "G2", 0), False, True)
         ts(R("el", 42, WC), R("G2", 0, 192), MID, A.add)
-        for lo, hi in chunks(plan["xchunk"], ()):
-            when("corners", lo / 512)
+        store = dict((hi, lo) for lo, hi in cut(plan["store"] if r else (TR,) * 3))
+        for lo, hi in cut(plan["corners"][r]):
+            when("corners", (lo - plan["turn"][r]) % M / 512)
             cp(R("O", lo, hi), ind(R("YO", 0, M + TR), R("xl", lo // 16, hi // 16)), "av")
-            if hi % plan["ochunk"] == 0:
-                lo = hi - plan["ochunk"]
+            if hi in store:
+                lo = store[hi]
                 at = (lo + 2 * TR) % M
                 dma((T.yx[:, at:at + hi - lo], []) if r else R("O2", lo, hi), R("O", lo, hi), 2 * (hi - lo))
         if r == 0:
@@ -605,18 +620,27 @@ def calls(core, rank, T, topo, plan):
             cp(R("U", 0, S), ind(R("WB", 0, W), R("el", 0, 42)), "av")
             compact(R("KK", 320, 362), "Bl", 0, S)
             ts(R("sl", 0, 42), R("KK", 320, 362), 7.5, A.add)
-            for p in range(3):
-                lo = S + p * TR
-                when("twins", p)
-                for a in range(lo, lo + TR, plan["wchunk"]):
-                    cp(R("U", a, a + plan["wchunk"]), ind(R("WB", 0, W), R("el", a // 16, (a + plan["wchunk"]) // 16)), "av")
-                compact(side("KK", p, at=128), "Bl", lo, lo + TR)
+            give(1)
+        first = len(ops)
+        for lo, hi in cut(plan["twins"][r]):
+            when("twins", lo / 512)
+            at = R("el", (S + lo) // 16, (S + hi) // 16)
+            if r == 1:
+                cp(R("SD", lo, hi), ind(R("SL", 0, W), at), "av")
+                dma((T.yt[:, lo:hi], []), R("SD", lo, hi, row=0), 1000, 1)
+                continue
+            cp(R("U", S + lo, S + hi), ind(R("WB", 0, W), at), "av")
+            if hi % TR == 0:
+                p = hi // TR - 1
+                compact(side("KK", p, at=128), "Bl", S + hi - TR, S + hi)
                 ts(side("dl", p), side("KK", p, at=128), 7.5, A.add)
-        else:
-            when("twins")
-            for lo, hi in chunks(plan["tchunk"], ()):
-                cp(R("SD", lo, hi), ind(R("SL", 0, W), R("el", (S + lo) // 16, (S + hi) // 16)), "av")
-                dma((T.yt[:, lo:hi], []), R("SD", lo, hi, row=0), 400, 1)
+        behind("twins%d" % r, first, ("O",))
+    early = [n for n, o in enumerate(ops) if o["kind"] == "c" and o["due"] < plan["early"] and not any(w[0] in ("TF", "TW", "dl", "WB", "give0", "SL", "A0", "A1") for w in o["w"])]
+    for n, o in enumerate(ops):
+        if o["alt"] == "g" and n in early:
+            o["behind"] = [m for m in early if m < n and ops[m]["alt"] == "g"]
+        if any(w[0] in ("give0", "SD") for w in o["w"]):
+            o["behind"] = [m for m in early if m < n] + o.get("also", [])
     link(ops)
     return ops
 

from concourse.bass import DstId, RemoteDMATransfer
from concourse.mybir import AluOpType as A, ActivationFunctionType as F

TR, M, S, C, N = 1024, 3072, 672, 96, 8
W = M + S
WC = W // 16
MID = 7.5 * WC
BIG = float(2 ** 25)
FAR = 32768.0
R16 = 1.5 * 2 ** 27
SCALES = [1.0, -1.0, float(WC), 1.0 / 16, 1024.0, -1024.0, 3072.0, -192.0]
LEAD = (16, M)
LISTS = ("sel", "hi", "dlo", "b16", "low")


def _sb(dt, **k):
    return {n: ("sbuf", [128] + (v if isinstance(v, list) else [v]), dt) for n, v in k.items()}


SCRATCH = {}
SCRATCH.update(_sb("bfloat16", O=W, O2=M, YO=M + TR, DM=M, come0=16 + S, come1=M + S, give0=S, give1=S, WB=W, U=W,
                   same=192, s16=96, s0=192, s2=192, cc=256, cl=240, tie=192, fl=192, dhi=192, LS=[len(LISTS), 240],
                   Ib=128 * len(SCALES), Bs=144, Bh=144, Bl=144))
SCRATCH.update(_sb("float16", PG=192, N1=192, N2=192, TS=192, MA=192, hh=192))
SCRATCH.update(_sb("float32", SD=M, SL=W, TF=[6, 2, 16], TW=192, f2=42, LOC=240, sm=192, Z=512, ZM=256, col=16, RD=256, RG=48, RB=256,
                   If=128, EE=128, GI=96, B0=144, f1=42))
SCRATCH.update(_sb("int32", TB=[2, 6, 16], SN=42, i1=42, P=12))
SCRATCH.update(_sb("uint16", dl=192, yl=192, xl=192, el=WC, sl=42, pl=64))
PSUM = ("A0", "A1", "G0", "G1", "G2", "KK", "S0", "S1")
for _n in PSUM:
    SCRATCH[_n] = ("psum", [128, 512], "float32")
NDMA = 40
SEMAPHORES = ["cv", "ca", "cp", "cg", "arr0", "arr1", "snt0", "snt1"] + ["d%d" % _k for _k in range(NDMA)]
SIX, FOUR = (512,) * 6, (1024, 1024, 512, 512)
PLAN = {
    "load": (2048, 1024), "loads": "sxxt", "twin": (FOUR, FOUR), "border": ("vvaaaa", "vvaaaa"), "corners": (SIX, SIX), "twins": (SIX, (512, 512, 512, 512, 384, 384, 256)),
    "store": (1024, 1024, 1024), "again": (0, 1, 2), "low": "v", "early": 3.2, "turn": (0, 0), "ask": (("av", "av"), ("av", "av")), "give": ((352, 320), (672,)), "rules": ("twins1",),
    "gat": 1.56, "mm": 0.004, "row": 0.023, "dma": 1.15, "rem": (3.0, 1.2), "remrows": 5.0, "wake": 0.07,
    "due": {"give": (0.3, 19.5, 0, 0), "digits": (8, 24, 0, 0), "slots": (11.0, 26.0, 0, 0), "rows": (11.0, 27.0, 0, 0),
            "same": (9, 26, 0, 0), "next": (12.5, 30.5, 0, 0), "prev": (13.6, 31.6, 0, 0), "edge": (2.5, 21.5, 0.6, 0.6),
            "sums": (6.0, 25.0, 1.0, 1.0), "twin": (5.7, 22.8, 0.7, 0.7), "key": (7.5, 26.5, 1.3, 1.3), "pos": (16.0, 34.0, 0, 0),
            "border": (14.0, 32.0, 0, 0), "flips": (13.5, 31.5, 0, 0), "lists": (18.0, 35.5, 0, 0),
            "corners": (18.3, 35.6, 0.2, 0.2), "sends": (18.1, 0, 0, 0), "twins": (21.3, 37.0, 0.5, 0.1)},
    "tries": 350000, "starts": 1, "cases": ((0.9, 0.9, 1.15, 1.0), (1.15, 1.05, 0.85, 1.05)), "seed": 65, "mean": 0.1, "heat": 0.35, "mark": 0.2, "reach": 30, "look": 0.1, "cold": 0, "lean": 0,
    "stones": ("sel", "xl", "YO")}
DEALT, WORTH = [], []


def meet(x, y):
    return x[0] == y[0] and x[1] < y[2] and y[1] < x[2] and (x[3] is None or y[3] is None or x[3] == y[3])


def link(ops):
    touch = {}
    for n, o in enumerate(ops):
        o["banks"] = set(r[0] for r in o["r"] + o["w"] if r[0] in PSUM)
        near = set()
        for r in o["r"] + o["w"]:
            near.update(touch.get(r[0], ()))
        o["pre"] = []
        for m in sorted(near):
            d = ops[m]
            raw = any(meet(x, y) for x in o["r"] for y in d["w"])
            war = any(meet(x, y) for x in o["w"] for y in d["w"] + d["r"])
            bank = bool(o["banks"] & d["banks"]) and not (o["alt"] == d["alt"] and o["alt"] in "va")
            if raw or war or bank:
                o["pre"].append((m, raw or war))
        for r in o["r"] + o["w"]:
            touch.setdefault(r[0], set()).add(n)


def play(ops, pre, order, at, plan, old=None, first=0):
    wake = plan["wake"]
    first -= first % 32
    if first:
        marks, done, by = old[2][:first // 32], list(old[3]), list(old[4])
        free, last = dict(old[2][first // 32][0]), dict(old[2][first // 32][1])
    else:
        marks, done, by = [], [0.0] * len(ops), [None] * len(ops)
        free, last = {e: 0.0 for e in "vapgsd"}, {e: None for e in "vapgsd"}
    for i in range(first, len(order)):
        if i % 32 == 0:
            marks.append((dict(free), dict(last)))
        n = order[i]
        c, lat, hold = ops[n]
        e = at[n]
        t, x, held = free[e], last[e], True
        for m in pre[n]:
            u = done[m] if e == "p" == at[m] else done[m] + wake
            if u > t:
                t, x, held = u, m, False
        if hold is None:
            done[n] = free[e] = t + c
        else:
            free[e] = t + hold
            if free["d"] > t + lat / 2:
                t, x, held = free["d"] - lat / 2, last["d"], True
            free["d"] = t + lat / 2 + c
            done[n] = t + lat + c
            last["d"] = n
        last[e] = n
        by[n] = (x, held)
    end = max(done)
    n, path = done.index(end), []
    while n is not None:
        path.append((n, by[n][0] if by[n][1] else None))
        n = by[n][0]
    return end + plan["mean"] * sum(done) / len(done) + plan["mark"] * sum(done[n] for n in plan["marks"]), path, marks, done, by


def deal(ops, plan):
    pre, above = [], []
    for o in ops:
        p = [m for m, _ in o["pre"]]
        far = set().union(*(above[m] for m in p))
        pre.append([m for m in p if m not in far])
        above.append(far.union(p, o.get("behind", ()), *(above[m] for m in o.get("behind", ()))))
    rank = [o["due"] for o in ops]
    for n in reversed(range(len(ops))):
        for m in pre[n] + list(ops[n].get("behind", ())):
            rank[m] = min(rank[m], rank[n] - 1e-6)
    order = sorted(range(len(ops)), key=lambda n: rank[n])
    at = [o["alt"][0] for o in ops]
    both = [len(o["alt"]) > 1 for o in ops]
    costs = [(o["c"], o["lat"], o["hold"]) for o in ops]
    if plan["look"]:
        order, done, since, free = [], {}, {}, {e: 0.0 for e in "vapgsd"}
        left = [set(pre[n]).union(o.get("behind", ())) for n, o in enumerate(ops)]
        after = [[] for _ in ops]
        for n, p in enumerate(left):
            for m in p:
                after[m].append(n)
        fresh, ready = [n for n, p in enumerate(left) if not p], []
        while fresh or ready:
            for n in fresh:
                since[n] = max([0.0] + [done[m] + plan["wake"] for m in pre[n]])
            ready = sorted(ready + fresh, key=lambda n: rank[n])
            pick = []
            for e in "vapgs":
                mine = [n for n in ready if e in ops[n]["alt"]
                        and not (e == "v" and both[n] and free["a"] <= max(free["v"], since[n]) + plan["lean"])]
                if mine:
                    t = max(free[e], min(since[n] for n in mine))
                    n = next(n for n in mine if since[n] <= t + plan["look"] * (8 if e == "g" else 1))
                    pick.append((t, rank[n], n, e))
            t, _, n, e = min(pick)
            t = max(t, since[n])
            c, lat, hold = costs[n]
            if hold is None:
                done[n] = free[e] = t + c
            else:
                free[e] = t + hold
                free["d"] = max(free["d"], t + lat / 2) + c
                done[n] = free["d"] + lat / 2
            at[n] = e
            order.append(n)
            ready.remove(n)
            for m in after[n]:
                left[m].discard(n)
            fresh = [m for m in after[n] if not left[m]]
    marks = [n for n, o in enumerate(ops) if o["kind"] == "rem" or any(w[0] in plan["stones"] for w in o["w"])]
    plan = dict(plan, marks=marks, mark=plan["mark"] / len(marks))
    cases = [[(c * (rows if o["kind"] == "rem" else gat if o.get("gather") else mm if o["alt"] == "p" else 1), lat * late, hold)
              for o, (c, lat, hold) in zip(ops, costs)] for rows, late, gat, mm in plan["cases"]]

    def plays(order, at, old, first):
        each = [play(c, pre, order, at, plan, old and old[1][k], first) for k, c in enumerate(cases)]
        return sum(x[0] for x in each) / len(each), each

    now = plays(order, at, None, 0)
    best = (now[0], order, at)
    seed = [plan["seed"]]

    def draw(k):
        seed[0] = (seed[0] * 1103515245 + 12345) % 2 ** 31
        return seed[0] // 256 % k

    begin = (now, order, at)
    for i in range(plan["tries"] * plan["starts"]):
        i %= plan["tries"]
        if i == 0:
            now, order, at = begin
        _, path, _, _, by = now[1][draw(len(cases))]
        if draw(2):
            n, path = marks[draw(len(marks))], []
            while n is not None and len(path) < plan["reach"]:
                path.append((n, by[n][0] if by[n][1] else None))
                n = by[n][0]
        n, m = path[draw(len(path))]
        k = draw(16)
        o2, a2 = order, at
        if k < 3:
            b = draw(len(ops))
            n = order[b]
            m = next((x for x in order[b - 1::-1] if at[x] == at[n]), None) if b else None
        if both[n] and k % 4 == 0:
            a = order.index(n)
            a2 = list(at)
            a2[n] = "a" if at[n] == "v" else "v"
            if k >= 8:
                near = [x for x in order[max(0, a - 25):a + 25] if both[x] and at[x] == a2[n]]
                if near:
                    a2[near[draw(len(near))]] = at[n]
                    a = max(0, a - 25)
        elif m is None or m in above[n]:
            continue
        else:
            a, b = order.index(m), order.index(n)
            if k % 2:
                front = [x == n or x in above[n] for x in order[a:b + 1]]
            else:
                front = [not (x == m or m in above[x]) for x in order[a:b + 1]]
            o2 = (order[:a] + [x for x, f in zip(order[a:b + 1], front) if f] + [x for x, f in zip(order[a:b + 1], front) if not f]
                  + order[b + 1:])
        new = plays(o2, a2, now, a)
        if new[0] <= now[0] + (k >= plan["cold"]) * plan["heat"] * (1 - i / plan["tries"]) * draw(8) / 8:
            now, order, at = new, o2, a2
            if now[0] < best[0]:
                best = (now[0], order, at)
    WORTH.append(best[0])
    return [(n, best[2][n]) for n in best[1]]


def emit(g, T, ops, order):
    q = {"v": g.vector, "a": g.scalar, "p": g.tensor, "g": g, "s": g.sync}
    know = {e: ({}, set()) for e in q}
    for n, (m, e) in enumerate(order):
        o = ops[m]; o["e"] = e; o["n"] = n; deps = []
        for x, raw in o["pre"]:
            d = ops[x]
            if d["kind"] == "rem" or (d["kind"] == "c" and o["kind"] == "c" and d["e"] == e and (e == "p" or not raw)):
                continue
            deps.append(d)
        clk, dm = know[e]; o["waits"] = []
        for d in sorted(deps, key=lambda d: -d["n"]):
            if (d["n"] in dm) if d["kind"] == "dma" else (clk.get(d["e"], -1) >= d["n"]):
                continue
            o["waits"].append(d); d["sig"] = True
            for k, v in d["clk"].items():
                clk[k] = max(clk.get(k, -1), v)
            dm.update(d["dm"])
        o["clk"] = dict(clk); o["dm"] = set(dm)
        if o["kind"] == "dma":
            o["dm"].add(n)
        else:
            o["clk"][e] = n
    count = {e: 0 for e in q}; nd = 0; seen = set()
    for m, e in order:
        o = ops[m]; best = {}
        for d in o["waits"]:
            best[d["at"][0]] = max(best.get(d["at"][0], 0), d["at"][1])
        for s, v in o["ext"]:
            if (e, s) not in seen:
                seen.add((e, s)); best[s] = v
        for s, v in best.items():
            q[e].wait_ge(T.sem[s], v)
        ins = o["fn"](q[e], e)
        if o["kind"] == "dma":
            o["at"] = ("d%d" % nd, 16); nd += 1
            ins.then_inc(T.sem[o["at"][0]], 16)
        elif o.get("sig"):
            count[e] += 1; o["at"] = ("c" + e, count[e])
            ins.then_inc(T.sem["c" + e], 1)
    for m, e in order:
        if ops[m]["kind"] == "dma" and not ops[m].get("sig"):
            g.sync.wait_ge(T.sem[ops[m]["at"][0]], 16)


def calls(core, rank, T, topo, plan):
    ops = []
    now = [0.0]

    def due(t):
        now[0] = t

    def R(name, lo, hi, step=1, row=None):
        if name in LISTS:
            return (T.LS[:, LISTS.index(name), lo:hi], [(name, lo, hi, None)], hi - lo, 2)
        part = slice(0, 128) if row is None else slice(row, 128, 16)
        ap = T[name][part, lo:hi] if step == 1 else T[name][part, lo:hi:step]
        return (ap, [(name, lo, hi, row)], len(range(lo, hi, step)), 4 if SCRATCH[name][2].endswith("32") else 2)

    def ind(win, off):
        return (win[0].indirect(off[0]), win[1] + off[1], 16 * off[2], 0)

    def add(e, kind, fn, w, r, c, lat=0.0, ext=()):
        ops.append({"alt": e, "kind": kind, "fn": fn, "w": list(w), "r": list(r), "ext": list(ext), "c": c, "lat": lat,
                    "due": now[0] + 1e-4 * len(ops), "hold": {"c": None, "dma": 0.05, "rem": lat - 0.7}[kind]})

    def cost(out, a, cycles=1.0):
        return 0.055 + 0.83e-3 * (plan["gat"] * a[2] if a[3] == 0 else max(64, out[2] * cycles))

    def tt(out, a, b, op, ext=()):
        both = a[1][0][0] not in PSUM and b[1][0][0] not in PSUM
        add("v", "c", lambda q, e: q.tensor_tensor(out[0], a[0], b[0], op), out[1], a[1] + b[1], cost(out, a, 2 if both else 1), 0.0, ext)
        ops[-1]["gather"] = a[3] == 0

    def ts(out, a, s1, op0, s2=None, op1=None):
        r = list(a[1]); v = []
        for s in (s1, s2):
            if isinstance(s, tuple):
                r += s[1]; v.append(s[0])
            else:
                v.append(s)
        c = cost(out, a, 0.5 if out[3] == a[3] == 2 else 1)
        if op1 is None:
            add("v", "c", lambda q, e: q.tensor_scalar(out[0], a[0], v[0], None, op0), out[1], r, c)
        else:
            add("v", "c", lambda q, e: q.tensor_scalar(out[0], a[0], v[0], v[1], op0, op1), out[1], r, c)

    def cp(out, a, e="v", ext=()):
        add(e, "c", lambda q, e: q.tensor_copy(out[0], a[0]) if e == "v" else q.activation(out[0], a[0], F.Copy), out[1], a[1],
            cost(out, a), 0.0, ext)
        ops[-1]["gather"] = a[3] == 0

    def square(out, a):
        add("a", "c", lambda q, e: q.activation(out[0], a[0], F.Square), out[1], a[1], cost(out, a))

    def relu(out, a):
        add("av", "c", lambda q, e: q.tensor_scalar(out[0], a[0], 0.0, None, A.max) if e == "v" else q.activation(out[0], a[0], F.Relu),
            out[1], a[1], cost(out, a))

    def affine(out, a, mul, plus):
        (m, rm), (b, rb) = ((s[0], s[1]) if isinstance(s, tuple) else (s, []) for s in (mul, plus))
        add("av", "c", lambda q, e: q.tensor_scalar(out[0], a[0], m, b, A.mult, A.add) if e == "v"
            else q.activation(out[0], a[0], F.Identity, bias=b, scale=m), out[1], a[1] + rm + rb, cost(out, a))

    def act(out, a, func, scale, bias):
        add("a", "c", lambda q, e: q.activation(out[0], a[0], func, bias=bias, scale=scale), out[1], a[1], cost(out, a))

    def group(out, terms, start=True, stop=True):
        def fn(q, e):
            for k, t in enumerate(terms):
                ins = q.matmul((t[2] if len(t) > 2 else out)[0], t[0][0], t[1][0], start and k == 0, stop and k == len(terms) - 1)
            return ins
        add("p", "c", fn, out[1], sum((t[0][1] + t[1][1] for t in terms), []),
            sum(plan["mm"] + 0.417e-3 * max(64, t[1][2]) * (4 if t[0][3] == 4 else 1) for t in terms))

    def iota(out, pat, base=0, cm=0, small=True):
        c = 0.13 + 1.66e-3 * out[2]
        if small:
            add("g", "c", lambda q, e: q.iota(out[0], pat, base, cm, allow_small_or_imprecise_dtypes=True), out[1], [], c)
        else:
            add("g", "c", lambda q, e: q.iota(out[0], pat, base, cm), out[1], [], c)

    def dma(out, a, row, rows=8):
        add("s", "dma", lambda q, e: q.dma_start(out[0], a[0]), out[1], a[1], rows * (plan["row"] + row / 22e3), plan["dma"])

    def side(name, p, n=64, at=0):
        return R(name, at + (p % 3) * n, at + (p % 3 + 1) * n)

    def cut(sizes):
        return [(sum(sizes[:k]), sum(sizes[:k + 1])) for k in range(len(sizes))]

    col = lambda k: R("col", k, k + 1)
    Ib = lambda k: R("Ib", 128 * k, 128 * k + 128)
    I1, IN, IW, I16, K1, KN, K3, N192 = (Ib(k) for k in range(len(SCALES)))
    IF = R("If", 0, 128)

    pieces = cut(plan["load"])
    for what in plan["loads"]:
        if what == "t":
            for gl in range(2):
                dma((T.TB[:, gl], [("TB", gl, gl + 1, None)]), (T.twn[gl:8:2, :], []), 384)
                ops[-1]["behind"] = range(len(ops) - 1)
        elif what == "s":
            dma(R("SN", 0, 42), (T.snd[:, :], []), 168)
        else:
            lo, hi = pieces.pop(0)
            dma(R("O", (lo + TR) % M, (lo + TR) % M + hi - lo), (T.x[:, lo:hi], []), 2 * (hi - lo))
        ops[-1]["behind"] = range(len(ops) - 1)
    for p in range(3):
        if p in plan["again"]:
            dma(side("WB", p, TR), (T.x[:, (p + 2) % 3 * TR:((p + 2) % 3 + 1) * TR], []), 2 * TR)
            ops[-1]["behind"] = range(len(ops) - 1)
        else:
            due(2.5 + (p - 1) % 3 * 0.5)
            add("v", "c", lambda q, e, p=p: q.tensor_copy(side("WB", p, TR)[0], side("O", p, TR)[0]), side("WB", p, TR)[1],
                side("O", p, TR)[1], 0.48)
            due(0.0)

    iota(R("P", 0, 1), [[0, 1]], 0, 1, small=False)
    iota(R("P", 1, 2), [[0, 1]], 0, 8, small=False)
    iota(R("RD", 0, 256), [[1, 256]])
    iota(R("RG", 0, 16), [[1, 8], [0, 2]])
    iota(R("RB", 0, 128), [[0, 8], [8, 2], [0, 8]])
    iota(R("cc", 0, 256), [[16, 256]])
    iota(R("tie", 0, 192), [[-1, 3], [0, 64]], -1)
    iota(R("come0", 0, 16), [[0, 16]], -256)
    iota(R("O", M, W), [[0, S]], int(FAR))
    add("v", "c", lambda q, e: q.memset(T.LS[:, :, 192:240], 0.0), [(nm, 192, 240, None) for nm in LISTS], [], 0.155)
    due(3.15)
    cp(R("WB", M, W), R("O", M, W), "av")
    due(1.0)
    ts(R("P", 2, 4), R("P", 0, 2), 4, A.arith_shift_right)
    ts(R("P", 4, 6), R("P", 0, 2), 15, A.bitwise_and)
    cp(R("col", 0, 6), R("P", 0, 6))
    ts(IF, R("RD", 0, 128), col(0), A.is_equal)
    for n, s in enumerate(SCALES):
        affine(Ib(n), IF, s, 0.0)
    ts(R("GI", 0, 16), R("RG", 0, 16), col(2), A.is_equal)
    affine(R("GI", 16, 32), R("GI", 0, 16), -1.0, 0.0)
    affine(col(9), col(4), 1.0, -7.5)
    affine(R("cl", 0, 240), R("RD", 0, 240), 0.0, col(9))
    affine(col(11), col(4), 1.0, -M / 2)
    ts(R("hh", 0, 192), R("cc", 0, 192), col(11), A.add)
    due(3.0)
    ts(R("ZM", 0, 128), R("RB", 0, 128), col(5), A.is_equal)
    ts(R("EE", 0, 64), R("RD", 0, 64), col(3), A.is_equal, 4.0, A.mult)
    due(11.0)
    affine(col(12), col(2), 16.0, 15.0)
    ts(R("B0", 0, 144), R("RD", 0, 144), col(12), A.is_equal)
    act(col(6), col(4), F.Relu, -1.0, 1.0)
    ts(col(7), col(4), 1.0, A.is_equal, float(WC), A.mult)
    ts(col(8), col(4), 2.0, A.is_equal, 1.0 / 16, A.mult)
    affine(col(7), col(8), 1.0, col(7))
    act(col(10), col(4), F.Abs, 1.0, -4.5)
    act(col(10), col(10), F.Relu, -1.0, 2.0)
    act(col(10), col(10), F.Sign, 1.0, 0.0)
    for nm, k in (("Bs", 6), ("Bh", 7), ("Bl", 10)):
        affine(R(nm, 0, 144), R("B0", 0, 144), col(k), 0.0)
    due(14.0)
    affine(R("LOC", 192, 240), R("RD", 192, 240), 16.0, col(4))

    due(0.5)
    for gl in range(2):
        add("v", "c", lambda q, e, gl=gl: q.tensor_scalar(T.TF[:, :, gl, :], T.TB[:, gl], -7.5, None, A.add),
            [("TF", 0, 2, gl)], [("TB", gl, gl + 1, None)], 0.13)
    for b in range(6):
        add("v", "c", lambda q, e, b=b: q.transpose(T.TW[:, b:192:6], T.TF[:, b]), [("TW", 0, 192, b)], [("TF", 0, 2, None)], 0.11)
    cp(R("sl", 0, 42), R("SN", 0, 42))
    ts(R("dl", 0, 192), R("TW", 0, 192), 7.5, A.add)
    due(12.0)
    ts(R("f1", 0, 42), R("SN", 0, 42), -7.5, A.add)
    act(R("f2", 0, 42), R("f1", 0, 42), F.Identity, 1.0, R16)
    act(R("s16", 0, 42), R("f2", 0, 42), F.Identity, 1.0, -R16)
    group(R("S1", 384, 426), [(IF, R("f1", 0, 42)), (IN, R("s16", 0, 42))])
    cp(R("s16", 48, 90), R("S1", 384, 426), "a")
    group(R("S1", 448, 490), [(I16, R("s16", 0, 42)), (IW, R("s16", 48, 90))])
    ts(R("el", 0, 42), R("S1", 448, 490), MID, A.add)

    PHI, TN = R("KK", 0, 64), R("G2", 320, 384)
    turned = lambda I, nm, to, at: [(I, R(nm, 0, 128), R(to, at + 64, at + 192)), (I, R(nm, 128, 192), R(to, at, at + 64))]
    key = lambda p: R("G%d" % p, 256, 320)
    OWN = (I1, R("hh", 0, 192))
    times = lambda k, a, to: [(K1 if k > 0 else KN, a, to)] * abs(k)
    stage = [0]

    def staging():
        stage[0] += 1
        return R("A%d" % (1 - stage[0] % 2), 0, 512)

    def reduce(p, first):
        nm, gi = ("SL", 0) if first else ("SD", 16)
        terms = [(R(nm, p * TR + j, (p + 1) * TR, 8), R("GI", gi, gi + 16), R("G%d" % p, j, 128, 8)) for j in range(8)]
        group(R("G%d" % p, 0, 128), terms, first, not first)

    def compact(out, B, lo, hi, more=()):
        group(out, list(more) + [(R(B, 15 - i, 143 - i), R("U", lo + i, hi, 16)) for i in range(16)])

    def give(r):
        due(plan["due"]["give"][r])
        for lo, hi in cut(plan["give"][r]):
            cp(R("give%d" % r, lo, hi), ind(R("O", 0, M), R("sl", lo // 16, hi // 16)), "va")
        trs = []
        for d in range(1, N):
            dst = T.cores[(rank + d) % N]
            rid, pid = topo.addr(dst, core)
            trs.append(RemoteDMATransfer(dst_ids=[DstId(rid=rid, pnc=pid)], dma_engine_mask=1 << topo.engines(core, dst)[d - 1],
                                         remote_sem=T.sem["arr%d" % r], src=T["give%d" % r][:, (d - 1) * C:d * C],
                                         dst=T["come%d" % r][:, LEAD[r] + (d - 1) * C:LEAD[r] + d * C]))
        add("g", "rem", lambda q, e, trs=trs, r=r: q.remote_dma_fused(trs, local_sem=T.sem["snt%d" % r]), [("arr%d" % r, 0, 1, None)],
            [("give%d" % r, 0, S, None)], plan["remrows"], plan["rem"][r])

    def behind(rule, first, names):
        if rule in plan["rules"]:
            for o in ops[first:]:
                o["behind"] = [n for n in range(first) if any(w[0] in names for w in ops[n]["w"])]

    give(0)
    due(6.0)
    first = len(ops)
    iota(R("come1", 0, M), [[0, M]], -256)
    iota(R("SL", M, W), [[0, S]])
    for n in range(first, len(ops)):
        ops[n]["behind"] = [n - 1]
    for r in range(2):
        TW = R("TW", 0, 192) if r == 0 else R("KK", 128, 320)
        come, yl = R("come%d" % r, 0, LEAD[r] + S), ("yl", "dl")[r]
        come = (come[0], come[1] + [("arr%d" % r, 0, 1, None)], come[2], come[3])
        arr = [("arr%d" % r, N - 1)]
        when = lambda step, k=0, r=r: due(plan["due"][step][r] + k * plan["due"][step][2 + r])
        when("digits")
        ts(R("b16", 0, 192), TW, R16, A.add, R16, A.subtract)
        if r == 0 and plan["low"] == "p":
            group(R("KK", 128, 320), [(IF, TW), (IN, R("b16", 0, 192))])
            cp(R("low", 0, 192), R("KK", 128, 320), "av")
        else:
            tt(R("low", 0, 192), TW, R("b16", 0, 192), A.subtract)
        ts(R("s0", 0, 192), R("b16", 0, 192), TR - 8.0, A.is_lt)
        ts(R("s2", 0, 192), R("b16", 0, 192), 2 * TR - 8.0, A.is_gt)
        when("slots")
        if r == 0:
            ts(R("yl", 0, 192), TW, 23.5 - M, A.add, 15.0, A.max)
        when("same")
        Z = R("KK", 320, 512)
        group(Z, [(IN, R("b16", 0, 192)), (IN, R("low", 0, 192)), (KN, R("s0", 0, 192)), (K1, R("s2", 0, 192))]
              + [(I1, side("hh", 1), side("KK", p, at=320)) for p in range(3)])
        ts(R("same", 0, 192), Z, 7.5 - M / 2, A.is_equal, -BIG, A.mult)
        when("next")
        group(R("S0", 256, 448), turned(IW, "low", "S0", 256) + turned(I16, "b16", "S0", 256) + turned(N192, "s2", "S0", 256))
        when("prev")
        at = 0 if r else 192
        low = [(IN, R("cl", 0, 192), R("S1", 0, 192))] + turned(I1, "low", "S1", 0)
        high = turned(I1, "b16", "S1", at) + turned(K3, "s0", "S1", at)
        high += [(IN, R("cc", 128, 192), side("S1", q)) for q in range(3)] if r else [(IN, R("cc", 64, 256), R("S1", 192, 384))]
        group(R("S1", 0, 384), low + high)
        for p in range(3):
            for h in range(2):
                when("edge", 2 * p + h)
                s = staging()
                group(s, [(I1, R("O", (p + 1) % 3 * TR + 512 * h, (p + 1) % 3 * TR + 512 * h + 512)),
                          (IN, R("O", (p + 2) % 3 * TR + 512 * h, (p + 2) % 3 * TR + 512 * h + 512))])
                square(R("SL", p * TR + 512 * h, p * TR + 512 * h + 512), s)
                if r == 0 and 2 * p + h > 0:
                    behind("give", len(ops) - 1, ("give0",))
            when("sums", p)
            reduce(p, True)
        for lo, hi in cut(plan["twin"][r]):
            when("twin", lo / 512)
            tt(R("SD", lo, hi), ind(R("O", 0, W), R("dl", lo // 16, hi // 16)), R("O2" if r else "WB", lo, hi), A.subtract)
            square(R("SD", lo, hi), R("SD", lo, hi))
            if r == 0 and "tail" in plan["rules"]:
                ops[-1]["also"] = [n for n, o in enumerate(ops) if ("WB", M, W, None) in o["w"]]
        when("rows")
        for row, nm in ((1, "low"), (2, "b16")):
            dma(R("WB", 0, W, row=row), R(nm, 0, WC), 468)
        for p in range(3):
            when("key", p)
            reduce(p, False)
            tt(side("Z", p, 128), R("G%d" % p, 0, 128), R("ZM", 0, 128), A.mult)
            group(key(p), [(I1, side("same", p)), (I1, side("tie", p))] + [(side("Z", p, 128), R("EE", 0, 64))])
            if p == 0:
                relu(side("sm", 0), key(0))
            else:
                tt(side("sm", p), key(p), side("sm", p - 1), A.max)
        for p in range(3):
            tt(side("sel", p + 1), key(p), side("sm", 2), A.is_equal)
        dma(R("WB", 0, W, row=0), R("sel", 0, WC), 468)
        tt(R("PG", 0, 192), R("S0", 256, 448), R("sel", 0, 192), A.mult)
        group(R("KK", 384, 448), [(I1, side("PG", p)) for p in range(3)])
        ts(R("pl", 0, 64), R("KK", 384, 448), MID + 64, A.add)
        for h in range(2):
            cp(R("U", 512 * h, 512 * h + 512), ind(R("WB", 0, W), R("pl", 32 * h, 32 * h + 32)), plan["ask"][r][h])
        if r == 0:
            dma(R("WB", 0, W, row=3), R("cc", 0, WC), 468)
            dma(R("WB", 0, W, row=4), R("cl", 0, WC), 468)
        compact(PHI, "Bs", 0, TR)
        compact(TN, "Bh", 0, TR)
        when("pos")
        group(R("S0", 0, 256), [(IW, R("low", 0, 192), R("S0", 0, 192)), (I16, R("b16", 0, 192), R("S0", 0, 192)),
                                (IW, R("low", 0, 64), R("S0", 192, 256)), (I16, R("b16", 0, 64), R("S0", 192, 256))])
        when("border")
        for n, e in enumerate(plan["border"][r]):
            lo, hi = 512 * n, 512 * n + 512
            if e == "v":
                tt(R("YO", lo, hi), ind(come, R(yl, lo // 16, hi // 16)), R("O", lo, hi), A.max, arr)
            else:
                cp(R("DM", lo, hi), ind(come, R(yl, lo // 16, hi // 16)), "a", arr)
                s = staging()
                group(s, [(I1, R("O", lo, hi))])
                tt(R("YO", lo, hi), s, R("DM", lo, hi), A.max)
        dma(R("YO", M, M + TR), R("YO", 0, TR), 2 * TR)
        fl = lambda q: side("fl", q)
        when("flips")
        group(R("G0", 0, 192), [OWN], True, False)
        if r:
            group(R("G1", 0, 192), [OWN], True, False)
        for q in range(3):
            tt(fl(q), PHI, side("sel", q), A.mult)
        more = lambda q: 1 - q % 3 if r else 0
        group(R("G0", 0, 192), sum((times((q + 1) % 3 - q + more(q + 1), fl(q + 1), side("G0", q)) + times(1 + more(q), fl(q), side("G0", q))
                                    + times((q + 1) % 3 - q, fl(q - 1), side("G0", q)) for q in range(3)), []), False, False)
        group(R("G1", 0, 192), sum((times((q - 1) % 3 - q, fl(q - 1), side("G1", q)) + times(more(q), fl(q), side("G1", q))
                                    for q in range(3)), []), r == 0, False)
        far = (("dhi", 192), ("dlo", 0)) if r == 0 else (("MA", 0),)
        for nm, at in far:
            tt(R(nm, 0, 192), R("S1", at, at + 192), R("fl", 0, 192), A.mult)
        group(R("G1", 0, 192), [(I1, R(far[0][0], 0, 192))], False, True)
        if r == 0:
            cp(R("hi", 0, 192), R("G1", 0, 192), "av")
            dma(R("WB", 0, W, row=5), R("dlo", 0, WC), 468)
            dma(R("WB", 0, W, row=6), R("hi", 0, WC), 468)
        else:
            affine(R("LOC", 0, 192), R("G1", 0, 192), 1.0, M / 2)
            dma(R("SL", 0, W, row=0), R("LOC", 0, WC), 936)
        group(R("G0", 0, 192), sum(([(I1, R(nm, 0, 192)), (I1, R(nm, 64, 192), R("G0", 0, 128)), (I1, R(nm, 0, 64), R("G0", 128, 192))]
                                    for nm, _ in far), []), False, True)
        ts(R("xl", 0, 192), R("G0", 0, 192), M / 2, A.add)
        when("lists")
        group(R("G2", 0, 192), [(IW, R("low", 0, 192)), (I16, R("b16", 0, 192))], True, False)
        first = len(ops)
        tt(R("N1", 0, 192), R("S0", 64, 256), R("fl", 0, 192), A.mult)
        tt(R("N2", 0, 192), R("S0", 0, 192), R("fl", 0, 192), A.mult)
        for q in range(3):
            tt(side("TS", q + 1), TN, fl(q), A.mult)
        behind("lists%d" % r, first, ("YO", "xl"))
        group(R("G2", 0, 192), [(I1, R("N1", 0, 192)), (IN, R("N2", 0, 192)), (I1, R("TS", 0, 192))] + turned(IN, "N1", "G2", 0), False, True)
        ts(R("el", 42, WC), R("G2", 0, 192), MID, A.add)
        store = dict((hi, lo) for lo, hi in cut(plan["store"] if r else (TR,) * 3))
        for lo, hi in cut(plan["corners"][r]):
            when("corners", (lo - plan["turn"][r]) % M / 512)
            cp(R("O", lo, hi), ind(R("YO", 0, M + TR), R("xl", lo // 16, hi // 16)), "av")
            if hi in store:
                lo = store[hi]
                at = (lo + 2 * TR) % M
                dma((T.yx[:, at:at + hi - lo], []) if r else R("O2", lo, hi), R("O", lo, hi), 2 * (hi - lo))
        if r == 0:
            when("sends")
            cp(R("U", 0, S), ind(R("WB", 0, W), R("el", 0, 42)), "av")
            compact(R("KK", 320, 362), "Bl", 0, S)
            ts(R("sl", 0, 42), R("KK", 320, 362), 7.5, A.add)
            give(1)
        first = len(ops)
        for lo, hi in cut(plan["twins"][r]):
            when("twins", lo / 512)
            at = R("el", (S + lo) // 16, (S + hi) // 16)
            if r == 1:
                cp(R("SD", lo, hi), ind(R("SL", 0, W), at), "av")
                dma((T.yt[:, lo:hi], []), R("SD", lo, hi, row=0), 1000, 1)
                continue
            cp(R("U", S + lo, S + hi), ind(R("WB", 0, W), at), "av")
            if hi % TR == 0:
                p = hi // TR - 1
                compact(side("KK", p, at=128), "Bl", S + hi - TR, S + hi)
                ts(side("dl", p), side("KK", p, at=128), 7.5, A.add)
        behind("twins%d" % r, first, ("O",))
    early = [n for n, o in enumerate(ops) if o["kind"] == "c" and o["due"] < plan["early"] and not any(w[0] in ("TF", "TW", "dl", "WB", "give0", "SL", "A0", "A1") for w in o["w"])]
    for n, o in enumerate(ops):
        if o["alt"] == "g" and n in early:
            o["behind"] = [m for m in early if m < n and ops[m]["alt"] == "g"]
        if any(w[0] in ("give0", "SD") for w in o["w"]):
            o["behind"] = [m for m in early if m < n] + o.get("also", [])
    link(ops)
    return ops


def rank_program(g, core, T, topo):
    rank = T.rank_of(core)
    if rank is None:
        return
    ops = calls(core, rank, T, topo, PLAN)
    if not DEALT:
        DEALT.extend(deal(ops, PLAN))
    emit(g, T, ops, DEALT)
    for r in range(2):
        g.wait_ge(T.sem["snt%d" % r], N - 1)
